import numpy as np
import ml_dtypes


def mxq(x, axis, fmt="e4m3"):
    dtype, down = {"e4m3": (ml_dtypes.float8_e4m3fn, 7), "e5m2": (ml_dtypes.float8_e5m2, 14)}[fmt]
    v = np.moveaxis(np.asarray(x, np.float32).astype(ml_dtypes.bfloat16).astype(np.float64), axis, -1)
    blocks = v.reshape(v.shape[:-1] + (-1, 32))
    amax = np.abs(blocks).max(-1, keepdims=True)
    byte = np.maximum(np.where(amax > 0, np.frexp(amax)[1] - 1 + 127, 0) - down, 1)
    scale = np.exp2(byte - 127.0)
    codes = (blocks / scale).astype(np.float32).astype(dtype).astype(np.float64)
    return np.moveaxis((codes * scale).reshape(v.shape), -1, axis)


WIDE = False


def mx_kscale(k):
    if not WIDE:
        return np.ones(k)
    levels = np.array([10, -10, 5, -5, 0])
    if k % 512:
        return np.exp2(np.random.permutation(np.resize(levels, k // 32))).repeat(32)
    a = np.empty((k // 512, 16))
    for p in range(k // 512):
        a[p, :8] = np.random.permutation(np.resize(levels, 8))
        for g in range(8):
            far = levels[np.abs(levels - a[p, g]) >= 10]
            a[p, g + 8] = far[np.random.randint(len(far))]
    return np.exp2(a.ravel()).repeat(32)


def f64(x):
    return np.asarray(x).astype(np.float64)


def striped(idx):
    return np.tile(idx.reshape(-1, 16).T, (8, 1)).astype(np.uint16)


def unstriped(offs):
    return offs[:16].T.reshape(-1).astype(np.int64)


E2M1 = np.array([0.0, 0.5, 1.0, 1.5, 2.0, 3.0, 4.0, 6.0, -0.0, -0.5, -1.0, -1.5, -2.0, -3.0, -4.0, -6.0])


def pack_weight(w, fmt):
    k, n = w.shape
    w = f64(np.asarray(w, np.float32).astype(ml_dtypes.bfloat16)).reshape(k // 32, 32, n)
    amax = np.abs(w).max(1)
    if fmt == "e4m3":
        byte = np.frexp(amax)[1] - 1 + 127 - 7
    else:
        mant, ex = np.frexp(amax / 6.0)
        byte = np.where(mant > 0.5, ex, ex - 1) + 127
    byte = np.clip(np.where(amax > 0, byte, 1), 1, 254)
    scaled = (w * np.exp2(127.0 - byte)[:, None, :]).reshape(k, n).astype(np.float32)
    by_word = np.ascontiguousarray(scaled.reshape(k // 512, 128, 4, n).transpose(0, 1, 3, 2))
    if fmt == "e4m3":
        words = by_word.astype(ml_dtypes.float8_e4m3fn).view(np.uint8)
    else:
        c = by_word.astype(ml_dtypes.float4_e2m1fn).view(np.uint8) & 0xF
        words = (c[..., 0::2] | (c[..., 1::2] << 4)).reshape(k // 512, 128, 2 * n)
    return np.ascontiguousarray(words), np.ascontiguousarray(byte.astype(np.uint8).reshape(k // 512, 16, n))


def unpack_weight(words, scales, fmt):
    g, _, n = scales.shape
    words = np.ascontiguousarray(words).reshape(g, 128, n, -1)
    if fmt == "e4m3":
        vals = words.view(ml_dtypes.float8_e4m3fn).astype(np.float64)
    else:
        nib = np.empty((g, 128, n, 4), np.uint8)
        nib[..., 0::2] = words & 0xF
        nib[..., 1::2] = words >> 4
        vals = E2M1[nib]
    vals = vals * np.repeat(np.exp2(scales.astype(np.float64) - 127.0), 8, axis=1)[..., None]
    return vals.transpose(0, 1, 3, 2).reshape(g * 512, n)


def gelu(v):
    return 0.5 * v * (1.0 + np.tanh(np.sqrt(2.0 / np.pi) * (v + 0.044715 * v**3)))


def bf(x):
    return np.asarray(x, np.float32).astype(ml_dtypes.bfloat16)

def planes(Y):
    n, m = Y.shape
    b = f64(bf(Y)).reshape(n // 32, 32, m)
    amax = np.abs(b).max(1)
    byte = np.clip(np.where(amax > 0, np.frexp(amax)[1] - 1 + 127 - 7, 1), 1, 254)
    codes = (b * np.exp2(127.0 - byte)[:, None, :]).reshape(n, m).astype(np.float32).astype(ml_dtypes.float8_e4m3fn).view(np.uint8)
    words = codes.reshape(n // 512, 128, 4, m).transpose(0, 1, 3, 2)
    return np.ascontiguousarray(words), np.ascontiguousarray(byte.astype(np.uint8).reshape(n // 512, 16, m))


K, K2, T, T2, S, H, N = 1024, 512, 2048, 4096, 1024, 512, 1024

def setup_inputs():
    n = np.random.standard_normal
    s = mx_kscale(K)[:, None]
    s2 = mx_kscale(K2)[:, None]
    u = mx_kscale(H)[:, None]
    tab_words, tab_scales = pack_weight(n((K, T)) * s, "e4m3")
    tab2_words, tab2_scales = pack_weight(n((K2, T2)) * s2, "e4m3")
    wa = (n((K, H)) / np.sqrt(K) / s * u.T).astype(np.float32)
    wb_words, wb_scales = pack_weight(n((K2, H)) / np.sqrt(K2) / s2 * u.T, "e2m1")
    gain = np.exp(0.8 * n(N))[None, :]
    wm_words, wm_scales = pack_weight(n((K2, N)) / np.sqrt(K2) / s2 * gain, "e4m3")
    we = (n((H, N)) / np.sqrt(H) / u).astype(np.float32)
    be = (0.5 * n(N)).astype(np.float32)
    gT = (0.05 + 0.6 * np.random.rand(H, T)).astype(np.float32)
    return {"tab_words": tab_words, "tab_scales": tab_scales,
            "tab2_words": tab2_words, "tab2_scales": tab2_scales,
            "wa": wa, "wb_words": wb_words, "wb_scales": wb_scales,
            "wm_words": wm_words, "wm_scales": wm_scales, "we": we, "be": be, "gT": gT,
            "offs": striped(np.random.permutation(T)[:S]),
            "offs2": striped(np.random.permutation(T2)[:S])}

def reference(tab_words, tab_scales, tab2_words, tab2_scales, wa, wb_words, wb_scales,
              wm_words, wm_scales, we, be, gT, offs, offs2):
    v = unpack_weight(tab_words, tab_scales, "e4m3")[:, unstriped(offs)]
    v2 = unpack_weight(tab2_words, tab2_scales, "e4m3")[:, unstriped(offs2)]
    g = f64(gT)[:, unstriped(offs)]
    wb = unpack_weight(wb_words, wb_scales, "e2m1")
    wm = unpack_weight(wm_words, wm_scales, "e4m3")
    z = mxq(f64(wa), 0, "e4m3").T @ v + wb.T @ v2
    h = np.maximum(z, g * z)
    e = mxq(f64(we), 0, "e4m3").T @ mxq(h, 0, "e4m3")
    m = wm.T @ v2
    a = 1.0 / (1.0 + np.exp(-(e + f64(be)[:, None])))
    y = a * m
    words, scales = planes(y)
    return y, words, scales

@@ -1,0 +1,254 @@
+from contextlib import ExitStack
+
+import concourse.mybir as mybir
+
+K, K2, T, T2, S, H, N = 1024, 512, 2048, 4096, 1024, 512, 1024
+FLOPS = 2 * S * (K * H + K2 * H + H * N + K2 * N)
+
+F32 = mybir.dt.float32
+BF16 = mybir.dt.bfloat16
+I32 = mybir.dt.int32
+U32 = mybir.dt.uint32
+U16 = mybir.dt.uint16
+U8 = mybir.dt.uint8
+FP8X4 = mybir.dt.float8_e4m3fn_x4
+FP4X4 = mybir.dt.float4_e2m1fn_x4
+MULT = mybir.AluOpType.mult
+MAX = mybir.AluOpType.max
+SIGMOID = mybir.ActivationFunctionType.Sigmoid
+
+P = 128
+PACK = 4
+PASS = P * PACK
+CHUNK = 512
+
+
+def tile_list_citation_edge_gate_kernel(
+    tc, tab_words, tab_scales, tab2_words, tab2_scales, wa, wb_words, wb_scales,
+    wm_words, wm_scales, we, be, gT, offs, offs2, out_0, out_1, out_2,
+):
+    nc = tc.nc
+    with ExitStack() as ctx:
+        keep = ctx.enter_context(tc.tile_pool(name="keep", bufs=1))
+        work = ctx.enter_context(tc.tile_pool(name="work", bufs=1))
+        psum = ctx.enter_context(tc.psum_pool(name="psum", bufs=1))
+
+        def held(shape, dtype, name):
+            return keep.tile(shape, dtype, name=name, align_bytes=64)
+
+        def words_of(dram, a):
+            return dram[a].rearrange("p t i -> p (t i)").bitcast(I32)
+
+        idx = keep.tile([P, S // 16], U16, name="idx")
+        idx2 = keep.tile([P, S // 16], U16, name="idx2")
+        tab_sc = held([P, T], U8, "tab_sc")
+        tab2_sc = held([P, T2], U8, "tab2_sc")
+        w_sc_raw = held([P, PASS], U8, "w_sc_raw")
+        nc.vector.memset(tab_sc[:].bitcast(I32), 0)
+        nc.vector.memset(tab2_sc[:].bitcast(I32), 0)
+        nc.vector.memset(w_sc_raw[:].bitcast(I32), 0)
+
+        def big(name, shape, dtype):
+            return work.tile(shape, dtype, name=name, tag="big", bufs=6, align_bytes=64)
+
+        tab_w = [big("tab_w%d" % a, [P, T], I32) for a in range(2)]
+        tab2_w = held([P, T2], I32, "tab2_w")
+        g_win = [held([P, T], F32, "g_win%d" % t) for t in range(PACK)]
+        wa_raw = [big("wa_raw%d" % a, [P, PACK, PASS], F32) for a in range(2)]
+        we_raw = [big("we_raw%d" % g, [P, PACK, PASS], F32) for g in range(2)]
+        wb_raw = held([P, 2 * H], U8, "wb_raw")
+        wm_raw = held([P, N], I32, "wm_raw")
+        bias = held([P, 2, PACK], F32, "bias")
+
+        half = T // 2
+        nc.sync.dma_start(idx[:], offs)
+        nc.sync.dma_start(wb_raw[:].bitcast(I32), wb_words[0].bitcast(I32))
+        for u in range(2):
+            nc.sync.dma_start(tab_w[0][:, u * half:(u + 1) * half], words_of(tab_words, 0)[:, u * half:(u + 1) * half])
+        nc.sync.dma_start(idx2[:], offs2)
+        nc.sync.dma_start(bias[:], be.rearrange("(g p t) -> p g t", g=2, t=PACK))
+        for u in range(2):
+            nc.sync.dma_start(tab_w[1][:, u * half:(u + 1) * half], words_of(tab_words, 1)[:, u * half:(u + 1) * half])
+        for q in range(4):
+            nc.sync.dma_start(tab_sc[32 * q:32 * q + 8, :].bitcast(I32), tab_scales[:, 4 * q:4 * q + 4, :].bitcast(I32))
+        wa_rows = wa.rearrange("(a p j) r -> a p j r", a=2, j=PACK)
+        g_rows = gT.rearrange("(p t) c -> t p c", t=PACK)
+        we_rows = we.rearrange("(p j) (g n) -> g p j n", j=PACK, g=2)
+        nc.sync.dma_start(wa_raw[0][:], wa_rows[0])
+        for q in range(4):
+            nc.sync.dma_start(tab2_sc[32 * q:32 * q + 4, :].bitcast(I32), tab2_scales[0, 4 * q:4 * q + 4, :].bitcast(I32))
+        nc.sync.dma_start(wa_raw[1][:], wa_rows[1])
+        for q in range(4):
+            nc.sync.dma_start(w_sc_raw[32 * q:32 * q + 4, :].bitcast(I32), wb_scales[0, 4 * q:4 * q + 4, :].bitcast(I32))
+        nc.sync.dma_start(tab2_w[:, :T], words_of(tab2_words, 0)[:, :T])
+        for q in range(4):
+            nc.sync.dma_start(
+                w_sc_raw[32 * q + 4:32 * q + 12, :].bitcast(I32),
+                wm_scales[0, 4 * q:4 * q + 4, :].bitcast(I32).rearrange("r (g n) -> g r n", g=2),
+            )
+        nc.sync.dma_start(tab2_w[:, T:], words_of(tab2_words, 0)[:, T:])
+        for t in range(PACK):
+            nc.sync.dma_start(g_win[t][:], g_rows[t])
+        for u in range(2):
+            nc.sync.dma_start(we_raw[0][:, :, u * 256:(u + 1) * 256], we_rows[0][:, :, u * 256:(u + 1) * 256])
+        nc.sync.dma_start(wm_raw[:], words_of(wm_words, 0))
+        nc.sync.dma_start(we_raw[1][:], we_rows[1])
+
+        wb_w = held([P, 2 * H], U8, "wb_w")
+        nc.vector.tensor_copy(
+            wb_w[:].rearrange("p (t m b) -> p m t b", t=PACK, b=2),
+            wb_raw[:].rearrange("p (m t b) -> p m t b", t=PACK, b=2),
+        )
+        v_w = [held([P, S], U32, "v_w%d" % a) for a in range(2)]
+        v_sc = held([P, S], U8, "v_sc")
+        v2_w = held([P, S], U32, "v2_w")
+        v2_sc = held([P, S], U8, "v2_sc")
+        for a in range(2):
+            nc.vector.tensor_copy(v_w[a][:], tab_w[a][:].bitcast(U32).indirect(idx[:]))
+        nc.vector.tensor_copy(v_sc[:], tab_sc[:].indirect(idx[:]))
+        nc.vector.tensor_copy(v2_sc[:], tab2_sc[:].indirect(idx2[:]))
+
+        def round_weight(raw, name, parts=1):
+            staged = work.tile([P, PASS * PACK], BF16, name=name, tag="staged", bufs=3, align_bytes=64)
+            for u in range(parts):
+                ms = slice(u * P // parts, (u + 1) * P // parts)
+                nc.scalar.copy(
+                    staged[:].rearrange("p (t m j) -> p m j t", t=PACK, j=PACK)[:, ms],
+                    raw[:].rearrange("p j (m t) -> p m j t", t=PACK)[:, ms],
+                )
+            return staged
+
+        def quantise(staged, name):
+            codes = held([P, PASS], U32, name + "_w")
+            scales = held([P, PASS], U8, name + "_sc")
+            nc.vector.quantize_mx(out=codes[:].bitcast(FP8X4), scales=scales[:], in_=staged)
+            return codes, scales
+
+        w_sc = held([P, PASS], U8, "w_sc")
+        nc.vector.tensor_copy(
+            w_sc[:].rearrange("p (t m) -> p m t", t=PACK),
+            w_sc_raw[:].rearrange("p (m t) -> p m t", t=PACK),
+        )
+        wa_q = [quantise(round_weight(wa_raw[a], "wa_bf%d" % a)[:], "wa_q%d" % a) for a in range(2)]
+        for c in range(2):
+            nc.vector.tensor_copy(
+                v2_w[:, c * CHUNK:(c + 1) * CHUNK],
+                tab2_w[:].bitcast(U32).indirect(idx2[:, c * CHUNK // 16:(c + 1) * CHUNK // 16]),
+            )
+
+        z_sb = [held([P, PACK, CHUNK], F32, "z_sb%d" % c) for c in range(2)]
+        gz6 = held([P, PACK + 2, CHUNK], F32, "gz6")
+        scratch = held([P, 2 * PACK, CHUNK], F32, "scratch")
+
+        def sloped(c):
+            return gz6[:, 2 - 2 * c:2 - 2 * c + PACK, :]
+
+        def first_product(c, t):
+            cols = slice(c * CHUNK, (c + 1) * CHUNK)
+            ms = slice(t * P, (t + 1) * P)
+            z = psum.tile([P, CHUNK], F32, name="z", tag="z", bufs=4)
+            for a in range(2):
+                nc.tensor.matmul_mx(
+                    out=z[:], lhsT=wa_q[a][0][:, ms].bitcast(FP8X4), lhsT_scale=wa_q[a][1][:, ms],
+                    rhs=v_w[a][:, cols].bitcast(FP8X4), rhs_scale=v_sc[4 * a:, cols],
+                    start=(a == 0), stop=False,
+                )
+            nc.tensor.matmul_mx(
+                out=z[:], lhsT=wb_w[:, 2 * t * P:2 * (t + 1) * P].bitcast(FP4X4), lhsT_scale=w_sc[:, ms],
+                rhs=v2_w[:, cols].bitcast(FP8X4), rhs_scale=v2_sc[:, cols],
+                start=False, stop=True,
+            )
+            nc.scalar.copy(z_sb[c][:, t, :], z[:])
+
+        def slope(c, t):
+            nc.vector.tensor_tensor(
+                sloped(c)[:, t, :], g_win[t][:].indirect(idx[:, c * CHUNK // 16:(c + 1) * CHUNK // 16]),
+                z_sb[c][:, t, :], MULT,
+            )
+
+        def rectify(c):
+            first = (1 - c) * PACK
+            h_bf = scratch[:, first:first + 2, :].rearrange("p s n -> p (s n)").bitcast(BF16)
+            nc.vector.tensor_tensor(
+                h_bf.rearrange("p (c i t) -> p c t i", i=2, t=PACK),
+                z_sb[c][:].rearrange("p t (c i) -> p c t i", i=2),
+                sloped(c).rearrange("p t (c i) -> p c t i", i=2),
+                MAX,
+            )
+            return quantise(h_bf, "h_q%d" % c)
+
+        for t in range(2):
+            for c in range(2):
+                first_product(c, t)
+        for c in range(2):
+            for t in range(2, PACK):
+                first_product(c, t)
+        for t in range(2):
+            for c in range(2):
+                slope(c, t)
+        for t in range(2, PACK):
+            slope(0, t)
+
+        y_w = [held([P, S], U32, "y_w%d" % g) for g in range(2)]
+        y_sc = held([P, 2, S], U8, "y_sc")
+        y_rows = out_0.rearrange("(g p t) j -> g t p j", g=2, t=PACK)
+
+        def second_stage(c, g, h_q, we_q, wm_w, round_on):
+            cols = slice(c * CHUNK, (c + 1) * CHUNK)
+            y = big("y", [P, PACK, CHUNK], F32)
+            for t in range(PACK):
+                ms = slice(t * P, (t + 1) * P)
+                e = psum.tile([P, CHUNK], F32, name="e", tag="e", bufs=2)
+                nc.tensor.matmul_mx(
+                    out=e[:], lhsT=we_q[0][:, ms].bitcast(FP8X4), lhsT_scale=we_q[1][:, ms],
+                    rhs=h_q[0][:].bitcast(FP8X4), rhs_scale=h_q[1][:], start=True, stop=True,
+                )
+                m = psum.tile([P, CHUNK], F32, name="m", tag="m", bufs=2)
+                nc.tensor.matmul_mx(
+                    out=m[:], lhsT=wm_w[:, g * PASS + t * P:g * PASS + (t + 1) * P].bitcast(FP8X4),
+                    lhsT_scale=w_sc[4 + 4 * g:, ms],
+                    rhs=v2_w[:, cols].bitcast(FP8X4), rhs_scale=v2_sc[:, cols], start=True, stop=True,
+                )
+                att = scratch[:, g * PACK + t, :]
+                nc.scalar.activation(att, e[:], SIGMOID, bias=bias[:, g, t:t + 1])
+                nc.vector.tensor_tensor(y[:, t, :], m[:], att, MULT)
+                nc.sync.dma_start(y_rows[g, t][:, cols], y[:, t, :])
+            width = CHUNK // len(round_on)
+            for u, rounder in enumerate(round_on):
+                part = slice(c * CHUNK + u * width, c * CHUNK + (u + 1) * width)
+                y_bf = work.tile([P, width, PACK], BF16, name="y_bf", tag="staged", bufs=3, align_bytes=64)
+                rounder(
+                    y_bf[:].rearrange("p (c i) t -> p c t i", i=4),
+                    y[:, :, u * width:(u + 1) * width].rearrange("p t (c i) -> p c t i", i=4),
+                )
+                nc.vector.quantize_mx(
+                    out=y_w[g][:, part].bitcast(FP8X4), scales=y_sc[:, g, part],
+                    in_=y_bf[:].rearrange("p c t -> p (c t)"),
+                )
+                nc.sync.dma_start(words_of(out_1, g)[:, part], y_w[g][:, part].bitcast(I32))
+
+        def store_scales(c, queue):
+            words = slice(c * CHUNK // 4, (c + 1) * CHUNK // 4)
+            for q in range(4):
+                queue.dma_start(
+                    out_2[:, 4 * q:4 * q + 4, :].bitcast(I32).rearrange("g r n -> r g n")[:, :, words],
+                    y_sc[32 * q:32 * q + 4, :, :].bitcast(I32)[:, :, words],
+                )
+
+        h_q0 = rectify(0)
+        we_q0 = quantise(round_weight(we_raw[0], "we_bf0", 2)[:], "we_q0")
+        wm_w = held([P, N], I32, "wm_w")
+        nc.vector.tensor_copy(
+            wm_w[:].rearrange("p (g t m) -> p g m t", g=2, t=PACK),
+            wm_raw[:].rearrange("p (g m t) -> p g m t", g=2, t=PACK),
+        )
+        for t in range(2, PACK):
+            slope(1, t)
+        second_stage(0, 0, h_q0, we_q0, wm_w, [nc.scalar.copy])
+        we_q1 = quantise(round_weight(we_raw[1], "we_bf1", 2)[:], "we_q1")
+        h_q1 = rectify(1)
+        second_stage(0, 1, h_q0, we_q1, wm_w, [nc.scalar.copy])
+        store_scales(0, nc.sync)
+        second_stage(1, 0, h_q1, we_q0, wm_w, [nc.scalar.copy])
+        second_stage(1, 1, h_q1, we_q1, wm_w, [nc.vector.tensor_copy, nc.vector.tensor_copy])
+        store_scales(1, nc.scalar)

@@ -96,8 +96,8 @@ def tile_list_citation_edge_gate_kernel(
 
         wb_w = held([P, 2 * H], U8, "wb_w")
         nc.vector.tensor_copy(
-            wb_w[:].rearrange("p (t m b) -> p m t b", t=PACK, b=2),
-            wb_raw[:].rearrange("p (m t b) -> p m t b", t=PACK, b=2),
+            wb_w[:].rearrange("p (t c i b) -> p c t i b", t=PACK, i=8, b=2),
+            wb_raw[:].rearrange("p (c i t b) -> p c t i b", t=PACK, i=8, b=2),
         )
         v_w = [held([P, S], U32, "v_w%d" % a) for a in range(2)]
         v_sc = held([P, S], U8, "v_sc")
@@ -113,8 +113,8 @@ def tile_list_citation_edge_gate_kernel(
             for u in range(parts):
                 ms = slice(u * P // parts, (u + 1) * P // parts)
                 nc.scalar.copy(
-                    staged[:].rearrange("p (t m j) -> p m j t", t=PACK, j=PACK)[:, ms],
-                    raw[:].rearrange("p j (m t) -> p m j t", t=PACK)[:, ms],
+                    staged[:].rearrange("p (t m j) -> p m t j", t=PACK, j=PACK)[:, ms],
+                    raw[:].rearrange("p j (m t) -> p m t j", t=PACK)[:, ms],
                 )
             return staged
 
@@ -126,8 +126,8 @@ def tile_list_citation_edge_gate_kernel(
 
         w_sc = held([P, PASS], U8, "w_sc")
         nc.vector.tensor_copy(
-            w_sc[:].rearrange("p (t m) -> p m t", t=PACK),
-            w_sc_raw[:].rearrange("p (m t) -> p m t", t=PACK),
+            w_sc[:].rearrange("p (t c i) -> p c t i", t=PACK, i=16),
+            w_sc_raw[:].rearrange("p (c i t) -> p c t i", t=PACK, i=16),
         )
         wa_q = [quantise(round_weight(wa_raw[a], "wa_bf%d" % a)[:], "wa_q%d" % a) for a in range(2)]
         for c in range(2):
@@ -138,7 +138,6 @@ def tile_list_citation_edge_gate_kernel(
 
         z_sb = [held([P, PACK, CHUNK], F32, "z_sb%d" % c) for c in range(2)]
         gz6 = held([P, PACK + 2, CHUNK], F32, "gz6")
-        scratch = held([P, 2 * PACK, CHUNK], F32, "scratch")
 
         def sloped(c):
             return gz6[:, 2 - 2 * c:2 - 2 * c + PACK, :]
@@ -167,8 +166,7 @@ def tile_list_citation_edge_gate_kernel(
             )
 
         def rectify(c):
-            first = (1 - c) * PACK
-            h_bf = scratch[:, first:first + 2, :].rearrange("p s n -> p (s n)").bitcast(BF16)
+            h_bf = work.tile([P, CHUNK * PACK], BF16, name="h_bf", tag="h_bf", bufs=2, align_bytes=64)[:]
             nc.vector.tensor_tensor(
                 h_bf.rearrange("p (c i t) -> p c t i", i=2, t=PACK),
                 z_sb[c][:].rearrange("p t (c i) -> p c t i", i=2),
@@ -177,11 +175,8 @@ def tile_list_citation_edge_gate_kernel(
             )
             return quantise(h_bf, "h_q%d" % c)
 
-        for t in range(2):
-            for c in range(2):
-                first_product(c, t)
         for c in range(2):
-            for t in range(2, PACK):
+            for t in range(PACK):
                 first_product(c, t)
         for t in range(2):
             for c in range(2):
@@ -189,30 +184,32 @@ def tile_list_citation_edge_gate_kernel(
         for t in range(2, PACK):
             slope(0, t)
 
-        y_w = [held([P, S], U32, "y_w%d" % g) for g in range(2)]
-        y_sc = held([P, 2, S], U8, "y_sc")
+        y_sc = [held([P, 2, CHUNK], U8, "y_sc%d" % c) for c in range(2)]
         y_rows = out_0.rearrange("(g p t) j -> g t p j", g=2, t=PACK)
 
-        def second_stage(c, g, h_q, we_q, wm_w, round_on):
+        def second_stage(c, g, h_q, we_q, wm_w):
             cols = slice(c * CHUNK, (c + 1) * CHUNK)
             y = big("y", [P, PACK, CHUNK], F32)
             for t in range(PACK):
                 ms = slice(t * P, (t + 1) * P)
-                e = psum.tile([P, CHUNK], F32, name="e", tag="e", bufs=2)
+                e = psum.tile([P, CHUNK], F32, name="e", tag="z", bufs=4)
                 nc.tensor.matmul_mx(
                     out=e[:], lhsT=we_q[0][:, ms].bitcast(FP8X4), lhsT_scale=we_q[1][:, ms],
                     rhs=h_q[0][:].bitcast(FP8X4), rhs_scale=h_q[1][:], start=True, stop=True,
                 )
-                m = psum.tile([P, CHUNK], F32, name="m", tag="m", bufs=2)
+                m = psum.tile([P, CHUNK], F32, name="m", tag="m", bufs=4)
                 nc.tensor.matmul_mx(
                     out=m[:], lhsT=wm_w[:, g * PASS + t * P:g * PASS + (t + 1) * P].bitcast(FP8X4),
                     lhsT_scale=w_sc[4 + 4 * g:, ms],
                     rhs=v2_w[:, cols].bitcast(FP8X4), rhs_scale=v2_sc[:, cols], start=True, stop=True,
                 )
-                att = scratch[:, g * PACK + t, :]
+                att = y[:, t, :]
                 nc.scalar.activation(att, e[:], SIGMOID, bias=bias[:, g, t:t + 1])
                 nc.vector.tensor_tensor(y[:, t, :], m[:], att, MULT)
                 nc.sync.dma_start(y_rows[g, t][:, cols], y[:, t, :])
+            return y
+
+        def planes(c, g, y, round_on):
             width = CHUNK // len(round_on)
             for u, rounder in enumerate(round_on):
                 part = slice(c * CHUNK + u * width, c * CHUNK + (u + 1) * width)
@@ -221,34 +218,39 @@ def tile_list_citation_edge_gate_kernel(
                     y_bf[:].rearrange("p (c i) t -> p c t i", i=4),
                     y[:, :, u * width:(u + 1) * width].rearrange("p t (c i) -> p c t i", i=4),
                 )
+                y_w = held([P, width], U32, "y_w%d%d%d" % (c, g, u))
                 nc.vector.quantize_mx(
-                    out=y_w[g][:, part].bitcast(FP8X4), scales=y_sc[:, g, part],
+                    out=y_w[:].bitcast(FP8X4), scales=y_sc[c][:, g, u * width:(u + 1) * width],
                     in_=y_bf[:].rearrange("p c t -> p (c t)"),
                 )
-                nc.sync.dma_start(words_of(out_1, g)[:, part], y_w[g][:, part].bitcast(I32))
+                nc.sync.dma_start(words_of(out_1, g)[:, part], y_w[:].bitcast(I32))
 
         def store_scales(c, queue):
             words = slice(c * CHUNK // 4, (c + 1) * CHUNK // 4)
             for q in range(4):
                 queue.dma_start(
                     out_2[:, 4 * q:4 * q + 4, :].bitcast(I32).rearrange("g r n -> r g n")[:, :, words],
-                    y_sc[32 * q:32 * q + 4, :, :].bitcast(I32)[:, :, words],
+                    y_sc[c][32 * q:32 * q + 4, :, :].bitcast(I32),
                 )
 
         h_q0 = rectify(0)
         we_q0 = quantise(round_weight(we_raw[0], "we_bf0", 2)[:], "we_q0")
         wm_w = held([P, N], I32, "wm_w")
         nc.vector.tensor_copy(
-            wm_w[:].rearrange("p (g t m) -> p g m t", g=2, t=PACK),
-            wm_raw[:].rearrange("p (g m t) -> p g m t", g=2, t=PACK),
+            wm_w[:].rearrange("p (g t c i) -> p g c t i", g=2, t=PACK, i=4),
+            wm_raw[:].rearrange("p (g c i t) -> p g c t i", g=2, t=PACK, i=4),
         )
         for t in range(2, PACK):
             slope(1, t)
-        second_stage(0, 0, h_q0, we_q0, wm_w, [nc.scalar.copy])
         we_q1 = quantise(round_weight(we_raw[1], "we_bf1", 2)[:], "we_q1")
         h_q1 = rectify(1)
-        second_stage(0, 1, h_q0, we_q1, wm_w, [nc.scalar.copy])
+        y00 = second_stage(0, 0, h_q0, we_q0, wm_w)
+        y01 = second_stage(0, 1, h_q0, we_q1, wm_w)
+        y10 = second_stage(1, 0, h_q1, we_q0, wm_w)
+        y11 = second_stage(1, 1, h_q1, we_q1, wm_w)
+        planes(0, 0, y00, [nc.scalar.copy])
+        planes(0, 1, y01, [nc.scalar.copy])
         store_scales(0, nc.sync)
-        second_stage(1, 0, h_q1, we_q0, wm_w, [nc.scalar.copy])
-        second_stage(1, 1, h_q1, we_q1, wm_w, [nc.vector.tensor_copy, nc.vector.tensor_copy])
+        planes(1, 1, y11, [nc.vector.tensor_copy])
+        planes(1, 0, y10, [nc.scalar.copy])
         store_scales(1, nc.scalar)

@@ -46,7 +46,7 @@ def tile_list_citation_edge_gate_kernel(
         w_sc_raw = held([P, PASS], U8, "w_sc_raw")
         nc.vector.memset(tab_sc[:].bitcast(I32), 0)
         nc.vector.memset(tab2_sc[:].bitcast(I32), 0)
-        nc.vector.memset(w_sc_raw[:].bitcast(I32), 0)
+        nc.gpsimd.memset(w_sc_raw[:].bitcast(I32), 0)
 
         def big(name, shape, dtype):
             return work.tile(shape, dtype, name=name, tag="big", bufs=6, align_bytes=64)
@@ -75,24 +75,23 @@ def tile_list_citation_edge_gate_kernel(
         g_rows = gT.rearrange("(p t) c -> t p c", t=PACK)
         we_rows = we.rearrange("(p j) (g n) -> g p j n", j=PACK, g=2)
         nc.sync.dma_start(wa_raw[0][:], wa_rows[0])
-        for q in range(4):
-            nc.sync.dma_start(tab2_sc[32 * q:32 * q + 4, :].bitcast(I32), tab2_scales[0, 4 * q:4 * q + 4, :].bitcast(I32))
+        for r in range(4):
+            nc.sync.dma_start(tab2_sc[r:P:32, :].bitcast(I32), tab2_scales[0, r:16:4, :].bitcast(I32))
         nc.sync.dma_start(wa_raw[1][:], wa_rows[1])
-        for q in range(4):
-            nc.sync.dma_start(w_sc_raw[32 * q:32 * q + 4, :].bitcast(I32), wb_scales[0, 4 * q:4 * q + 4, :].bitcast(I32))
+        for r in range(4):
+            nc.sync.dma_start(w_sc_raw[r:P:32, :].bitcast(I32), wb_scales[0, r:16:4, :].bitcast(I32))
         nc.sync.dma_start(tab2_w[:, :T], words_of(tab2_words, 0)[:, :T])
         for q in range(4):
-            nc.sync.dma_start(
+            nc.gpsimd.dma_start(
                 w_sc_raw[32 * q + 4:32 * q + 12, :].bitcast(I32),
                 wm_scales[0, 4 * q:4 * q + 4, :].bitcast(I32).rearrange("r (g n) -> g r n", g=2),
             )
         nc.sync.dma_start(tab2_w[:, T:], words_of(tab2_words, 0)[:, T:])
         for t in range(PACK):
             nc.sync.dma_start(g_win[t][:], g_rows[t])
-        for u in range(2):
-            nc.sync.dma_start(we_raw[0][:, :, u * 256:(u + 1) * 256], we_rows[0][:, :, u * 256:(u + 1) * 256])
-        nc.sync.dma_start(wm_raw[:], words_of(wm_words, 0))
+        nc.sync.dma_start(we_raw[0][:], we_rows[0])
         nc.sync.dma_start(we_raw[1][:], we_rows[1])
+        nc.sync.dma_start(wm_raw[:], words_of(wm_words, 0))
 
         wb_w = held([P, 2 * H], U8, "wb_w")
         nc.vector.tensor_copy(
@@ -108,13 +107,14 @@ def tile_list_citation_edge_gate_kernel(
         nc.vector.tensor_copy(v_sc[:], tab_sc[:].indirect(idx[:]))
         nc.vector.tensor_copy(v2_sc[:], tab2_sc[:].indirect(idx2[:]))
 
-        def round_weight(raw, name, parts=1):
-            staged = work.tile([P, PASS * PACK], BF16, name=name, tag="staged", bufs=3, align_bytes=64)
-            for u in range(parts):
-                ms = slice(u * P // parts, (u + 1) * P // parts)
+        def staging(name):
+            return work.tile([P, PASS * PACK], BF16, name=name, tag="staged", bufs=3, align_bytes=64)[:]
+
+        def round_weight(raw, staged):
+            for u in range(2):
                 nc.scalar.copy(
-                    staged[:].rearrange("p (t m j) -> p m t j", t=PACK, j=PACK)[:, ms],
-                    raw[:].rearrange("p j (m t) -> p m t j", t=PACK)[:, ms],
+                    staged.rearrange("p (u e m j) -> p u m j e", u=2, e=2, j=PACK)[:, u],
+                    raw[:].rearrange("p j (m u e) -> p u m j e", u=2, e=2)[:, u],
                 )
             return staged
 
@@ -129,7 +129,7 @@ def tile_list_citation_edge_gate_kernel(
             w_sc[:].rearrange("p (t c i) -> p c t i", t=PACK, i=16),
             w_sc_raw[:].rearrange("p (c i t) -> p c t i", t=PACK, i=16),
         )
-        wa_q = [quantise(round_weight(wa_raw[a], "wa_bf%d" % a)[:], "wa_q%d" % a) for a in range(2)]
+        wa_q = [quantise(round_weight(wa_raw[a], staging("wa_bf%d" % a)), "wa_q%d" % a) for a in range(2)]
         for c in range(2):
             nc.vector.tensor_copy(
                 v2_w[:, c * CHUNK:(c + 1) * CHUNK],
@@ -137,10 +137,10 @@ def tile_list_citation_edge_gate_kernel(
             )
 
         z_sb = [held([P, PACK, CHUNK], F32, "z_sb%d" % c) for c in range(2)]
-        gz6 = held([P, PACK + 2, CHUNK], F32, "gz6")
+        gz8 = held([P, 2 * PACK, CHUNK], F32, "gz8")
 
         def sloped(c):
-            return gz6[:, 2 - 2 * c:2 - 2 * c + PACK, :]
+            return gz8[:, c * PACK:(c + 1) * PACK, :]
 
         def first_product(c, t):
             cols = slice(c * CHUNK, (c + 1) * CHUNK)
@@ -165,8 +165,7 @@ def tile_list_citation_edge_gate_kernel(
                 z_sb[c][:, t, :], MULT,
             )
 
-        def rectify(c):
-            h_bf = work.tile([P, CHUNK * PACK], BF16, name="h_bf", tag="h_bf", bufs=2, align_bytes=64)[:]
+        def rectify(c, h_bf):
             nc.vector.tensor_tensor(
                 h_bf.rearrange("p (c i t) -> p c t i", i=2, t=PACK),
                 z_sb[c][:].rearrange("p t (c i) -> p c t i", i=2),
@@ -215,8 +214,8 @@ def tile_list_citation_edge_gate_kernel(
                 part = slice(c * CHUNK + u * width, c * CHUNK + (u + 1) * width)
                 y_bf = work.tile([P, width, PACK], BF16, name="y_bf", tag="staged", bufs=3, align_bytes=64)
                 rounder(
-                    y_bf[:].rearrange("p (c i) t -> p c t i", i=4),
-                    y[:, :, u * width:(u + 1) * width].rearrange("p t (c i) -> p c t i", i=4),
+                    y_bf[:].rearrange("p (c i) t -> p c t i", i=2),
+                    y[:, :, u * width:(u + 1) * width].rearrange("p t (c i) -> p c t i", i=2),
                 )
                 y_w = held([P, width], U32, "y_w%d%d%d" % (c, g, u))
                 nc.vector.quantize_mx(
@@ -233,8 +232,8 @@ def tile_list_citation_edge_gate_kernel(
                     y_sc[c][32 * q:32 * q + 4, :, :].bitcast(I32),
                 )
 
-        h_q0 = rectify(0)
-        we_q0 = quantise(round_weight(we_raw[0], "we_bf0", 2)[:], "we_q0")
+        h_q0 = rectify(0, staging("h_bf0"))
+        we_q0 = quantise(round_weight(we_raw[0], sloped(1)[:, 2:4, :].rearrange("p t n -> p (t n)").bitcast(BF16)), "we_q0")
         wm_w = held([P, N], I32, "wm_w")
         nc.vector.tensor_copy(
             wm_w[:].rearrange("p (g t c i) -> p g c t i", g=2, t=PACK, i=4),
@@ -242,8 +241,9 @@ def tile_list_citation_edge_gate_kernel(
         )
         for t in range(2, PACK):
             slope(1, t)
-        we_q1 = quantise(round_weight(we_raw[1], "we_bf1", 2)[:], "we_q1")
-        h_q1 = rectify(1)
+        shared = staging("we_bf1_then_h_bf1")
+        we_q1 = quantise(round_weight(we_raw[1], shared), "we_q1")
+        h_q1 = rectify(1, shared)
         y00 = second_stage(0, 0, h_q0, we_q0, wm_w)
         y01 = second_stage(0, 1, h_q0, we_q1, wm_w)
         y10 = second_stage(1, 0, h_q1, we_q0, wm_w)
@@ -252,5 +252,5 @@ def tile_list_citation_edge_gate_kernel(
         planes(0, 1, y01, [nc.scalar.copy])
         store_scales(0, nc.sync)
         planes(1, 1, y11, [nc.vector.tensor_copy])
-        planes(1, 0, y10, [nc.scalar.copy])
+        planes(1, 0, y10, [nc.scalar.copy, nc.scalar.copy])
         store_scales(1, nc.scalar)

@@ -15,6 +15,7 @@ FP8X4 = mybir.dt.float8_e4m3fn_x4
 FP4X4 = mybir.dt.float4_e2m1fn_x4
 MULT = mybir.AluOpType.mult
 MAX = mybir.AluOpType.max
+ADD = mybir.AluOpType.add
 SIGMOID = mybir.ActivationFunctionType.Sigmoid
 
 P = 128
@@ -137,10 +138,10 @@ def tile_list_citation_edge_gate_kernel(
             )
 
         z_sb = [held([P, PACK, CHUNK], F32, "z_sb%d" % c) for c in range(2)]
-        gz8 = held([P, 2 * PACK, CHUNK], F32, "gz8")
+        gz9 = held([P, 2 * PACK + 1, CHUNK], F32, "gz9")
 
         def sloped(c):
-            return gz8[:, c * PACK:(c + 1) * PACK, :]
+            return gz9[:, c * PACK:(c + 1) * PACK, :]
 
         def first_product(c, t):
             cols = slice(c * CHUNK, (c + 1) * CHUNK)
@@ -177,13 +178,12 @@ def tile_list_citation_edge_gate_kernel(
         for c in range(2):
             for t in range(PACK):
                 first_product(c, t)
-        for t in range(2):
+        for t in range(PACK - 1):
             for c in range(2):
                 slope(c, t)
-        for t in range(2, PACK):
-            slope(0, t)
+        slope(0, PACK - 1)
 
-        y_sc = [held([P, 2, CHUNK], U8, "y_sc%d" % c) for c in range(2)]
+        y_sc = held([P, 2, S], U8, "y_sc")
         y_rows = out_0.rearrange("(g p t) j -> g t p j", g=2, t=PACK)
 
         def second_stage(c, g, h_q, we_q, wm_w):
@@ -219,38 +219,41 @@ def tile_list_citation_edge_gate_kernel(
                 )
                 y_w = held([P, width], U32, "y_w%d%d%d" % (c, g, u))
                 nc.vector.quantize_mx(
-                    out=y_w[:].bitcast(FP8X4), scales=y_sc[c][:, g, u * width:(u + 1) * width],
+                    out=y_w[:].bitcast(FP8X4), scales=y_sc[:, g, part],
                     in_=y_bf[:].rearrange("p c t -> p (c t)"),
                 )
                 nc.sync.dma_start(words_of(out_1, g)[:, part], y_w[:].bitcast(I32))
 
-        def store_scales(c, queue):
-            words = slice(c * CHUNK // 4, (c + 1) * CHUNK // 4)
-            for q in range(4):
-                queue.dma_start(
-                    out_2[:, 4 * q:4 * q + 4, :].bitcast(I32).rearrange("g r n -> r g n")[:, :, words],
-                    y_sc[c][32 * q:32 * q + 4, :, :].bitcast(I32),
-                )
-
         h_q0 = rectify(0, staging("h_bf0"))
-        we_q0 = quantise(round_weight(we_raw[0], sloped(1)[:, 2:4, :].rearrange("p t n -> p (t n)").bitcast(BF16)), "we_q0")
+        we_q0 = quantise(round_weight(we_raw[0], gz9[:, 2 * PACK - 1:, :].rearrange("p t n -> p (t n)").bitcast(BF16)), "we_q0")
         wm_w = held([P, N], I32, "wm_w")
         nc.vector.tensor_copy(
             wm_w[:].rearrange("p (g t c i) -> p g c t i", g=2, t=PACK, i=4),
             wm_raw[:].rearrange("p (g c i t) -> p g c t i", g=2, t=PACK, i=4),
         )
-        for t in range(2, PACK):
-            slope(1, t)
-        shared = staging("we_bf1_then_h_bf1")
+        slope(1, PACK - 1)
+        y_bf0 = held([P, 2, CHUNK * PACK], BF16, "y_bf0")
+        shared = y_bf0[:, 0, :]
         we_q1 = quantise(round_weight(we_raw[1], shared), "we_q1")
         h_q1 = rectify(1, shared)
         y00 = second_stage(0, 0, h_q0, we_q0, wm_w)
         y01 = second_stage(0, 1, h_q0, we_q1, wm_w)
         y10 = second_stage(1, 0, h_q1, we_q0, wm_w)
         y11 = second_stage(1, 1, h_q1, we_q1, wm_w)
-        planes(0, 0, y00, [nc.scalar.copy])
+        for c, y in enumerate((y00, y10)):
+            nc.gpsimd.tensor_scalar(
+                y_bf0[:, c, :].rearrange("p (c t) -> p c t", t=PACK), y[:].rearrange("p t c -> p c t"),
+                1.0, 0.0, MULT, ADD,
+            )
+        y_w0 = held([P, S], U32, "y_w0")
+        nc.vector.quantize_mx(
+            out=y_w0[:].bitcast(FP8X4), scales=y_sc[:, 0, :], in_=y_bf0[:].rearrange("p c n -> p (c n)"),
+        )
+        nc.sync.dma_start(words_of(out_1, 0), y_w0[:].bitcast(I32))
         planes(0, 1, y01, [nc.scalar.copy])
-        store_scales(0, nc.sync)
-        planes(1, 1, y11, [nc.vector.tensor_copy])
-        planes(1, 0, y10, [nc.scalar.copy, nc.scalar.copy])
-        store_scales(1, nc.scalar)
+        planes(1, 1, y11, [nc.scalar.copy, nc.scalar.copy])
+        for q in range(4):
+            nc.scalar.dma_start(
+                out_2[:, 4 * q:4 * q + 4, :].bitcast(I32).rearrange("g r n -> r g n"),
+                y_sc[32 * q:32 * q + 4, :, :].bitcast(I32),
+            )

@@ -88,16 +88,20 @@ def tile_list_citation_edge_gate_kernel(
                 wm_scales[0, 4 * q:4 * q + 4, :].bitcast(I32).rearrange("r (g n) -> g r n", g=2),
             )
         nc.sync.dma_start(tab2_w[:, T:], words_of(tab2_words, 0)[:, T:])
-        for t in range(PACK):
+        for t in range(PACK - 1):
             nc.sync.dma_start(g_win[t][:], g_rows[t])
+        nc.sync.dma_start(wm_raw[:], words_of(wm_words, 0))
+        nc.sync.dma_start(g_win[PACK - 1][:], g_rows[PACK - 1])
         nc.sync.dma_start(we_raw[0][:], we_rows[0])
         nc.sync.dma_start(we_raw[1][:], we_rows[1])
-        nc.sync.dma_start(wm_raw[:], words_of(wm_words, 0))
+
+        warm = held([P, 1], F32, "warm")
+        nc.scalar.activation(warm[:], bias[:, 0, 0:1], SIGMOID)
 
         wb_w = held([P, 2 * H], U8, "wb_w")
         nc.vector.tensor_copy(
-            wb_w[:].rearrange("p (t c i b) -> p c t i b", t=PACK, i=8, b=2),
-            wb_raw[:].rearrange("p (c i t b) -> p c t i b", t=PACK, i=8, b=2),
+            wb_w[:].bitcast(U16).rearrange("p (t c i) -> p c t i", t=PACK, i=8),
+            wb_raw[:].bitcast(U16).rearrange("p (c i t) -> p c t i", t=PACK, i=8),
         )
         v_w = [held([P, S], U32, "v_w%d" % a) for a in range(2)]
         v_sc = held([P, S], U8, "v_sc")
@@ -138,31 +142,36 @@ def tile_list_citation_edge_gate_kernel(
             )
 
         z_sb = [held([P, PACK, CHUNK], F32, "z_sb%d" % c) for c in range(2)]
-        gz9 = held([P, 2 * PACK + 1, CHUNK], F32, "gz9")
+        gz = [held([P, PACK, CHUNK], F32, "gz%d" % c) for c in range(2)]
 
-        def sloped(c):
-            return gz9[:, c * PACK:(c + 1) * PACK, :]
+        def bank(name, c, width):
+            return psum.tile([P, width], F32, name=name, tag="bank%d" % c, bufs=4)
 
-        def first_product(c, t):
-            cols = slice(c * CHUNK, (c + 1) * CHUNK)
+        z = [[bank("z", c, CHUNK) for t in range(PACK)] for c in range(2)]
+        for a in range(2):
+            for c in range(2):
+                cols = slice(c * CHUNK, (c + 1) * CHUNK)
+                for t in range(PACK):
+                    ms = slice(t * P, (t + 1) * P)
+                    nc.tensor.matmul_mx(
+                        out=z[c][t][:], lhsT=wa_q[a][0][:, ms].bitcast(FP8X4), lhsT_scale=wa_q[a][1][:, ms],
+                        rhs=v_w[a][:, cols].bitcast(FP8X4), rhs_scale=v_sc[4 * a:, cols],
+                        start=(a == 0), stop=False,
+                    )
+        for t in range(PACK):
             ms = slice(t * P, (t + 1) * P)
-            z = psum.tile([P, CHUNK], F32, name="z", tag="z", bufs=4)
-            for a in range(2):
+            for c in range(2):
+                cols = slice(c * CHUNK, (c + 1) * CHUNK)
                 nc.tensor.matmul_mx(
-                    out=z[:], lhsT=wa_q[a][0][:, ms].bitcast(FP8X4), lhsT_scale=wa_q[a][1][:, ms],
-                    rhs=v_w[a][:, cols].bitcast(FP8X4), rhs_scale=v_sc[4 * a:, cols],
-                    start=(a == 0), stop=False,
+                    out=z[c][t][:], lhsT=wb_w[:, 2 * t * P:2 * (t + 1) * P].bitcast(FP4X4), lhsT_scale=w_sc[:, ms],
+                    rhs=v2_w[:, cols].bitcast(FP8X4), rhs_scale=v2_sc[:, cols],
+                    start=False, stop=True,
                 )
-            nc.tensor.matmul_mx(
-                out=z[:], lhsT=wb_w[:, 2 * t * P:2 * (t + 1) * P].bitcast(FP4X4), lhsT_scale=w_sc[:, ms],
-                rhs=v2_w[:, cols].bitcast(FP8X4), rhs_scale=v2_sc[:, cols],
-                start=False, stop=True,
-            )
-            nc.scalar.copy(z_sb[c][:, t, :], z[:])
+                nc.scalar.copy(z_sb[c][:, t, :], z[c][t][:])
 
         def slope(c, t):
             nc.vector.tensor_tensor(
-                sloped(c)[:, t, :], g_win[t][:].indirect(idx[:, c * CHUNK // 16:(c + 1) * CHUNK // 16]),
+                gz[c][:, t, :], g_win[t][:].indirect(idx[:, c * CHUNK // 16:(c + 1) * CHUNK // 16]),
                 z_sb[c][:, t, :], MULT,
             )
 
@@ -170,88 +179,86 @@ def tile_list_citation_edge_gate_kernel(
             nc.vector.tensor_tensor(
                 h_bf.rearrange("p (c i t) -> p c t i", i=2, t=PACK),
                 z_sb[c][:].rearrange("p t (c i) -> p c t i", i=2),
-                sloped(c).rearrange("p t (c i) -> p c t i", i=2),
+                gz[c][:].rearrange("p t (c i) -> p c t i", i=2),
                 MAX,
             )
-            return quantise(h_bf, "h_q%d" % c)
+            return h_bf
 
-        for c in range(2):
-            for t in range(PACK):
-                first_product(c, t)
         for t in range(PACK - 1):
             for c in range(2):
                 slope(c, t)
-        slope(0, PACK - 1)
-
-        y_sc = held([P, 2, S], U8, "y_sc")
-        y_rows = out_0.rearrange("(g p t) j -> g t p j", g=2, t=PACK)
-
-        def second_stage(c, g, h_q, we_q, wm_w):
-            cols = slice(c * CHUNK, (c + 1) * CHUNK)
-            y = big("y", [P, PACK, CHUNK], F32)
-            for t in range(PACK):
-                ms = slice(t * P, (t + 1) * P)
-                e = psum.tile([P, CHUNK], F32, name="e", tag="z", bufs=4)
-                nc.tensor.matmul_mx(
-                    out=e[:], lhsT=we_q[0][:, ms].bitcast(FP8X4), lhsT_scale=we_q[1][:, ms],
-                    rhs=h_q[0][:].bitcast(FP8X4), rhs_scale=h_q[1][:], start=True, stop=True,
-                )
-                m = psum.tile([P, CHUNK], F32, name="m", tag="m", bufs=4)
-                nc.tensor.matmul_mx(
-                    out=m[:], lhsT=wm_w[:, g * PASS + t * P:g * PASS + (t + 1) * P].bitcast(FP8X4),
-                    lhsT_scale=w_sc[4 + 4 * g:, ms],
-                    rhs=v2_w[:, cols].bitcast(FP8X4), rhs_scale=v2_sc[:, cols], start=True, stop=True,
-                )
-                att = y[:, t, :]
-                nc.scalar.activation(att, e[:], SIGMOID, bias=bias[:, g, t:t + 1])
-                nc.vector.tensor_tensor(y[:, t, :], m[:], att, MULT)
-                nc.sync.dma_start(y_rows[g, t][:, cols], y[:, t, :])
-            return y
-
-        def planes(c, g, y, round_on):
-            width = CHUNK // len(round_on)
-            for u, rounder in enumerate(round_on):
-                part = slice(c * CHUNK + u * width, c * CHUNK + (u + 1) * width)
-                y_bf = work.tile([P, width, PACK], BF16, name="y_bf", tag="staged", bufs=3, align_bytes=64)
-                rounder(
-                    y_bf[:].rearrange("p (c i) t -> p c t i", i=2),
-                    y[:, :, u * width:(u + 1) * width].rearrange("p t (c i) -> p c t i", i=2),
-                )
-                y_w = held([P, width], U32, "y_w%d%d%d" % (c, g, u))
-                nc.vector.quantize_mx(
-                    out=y_w[:].bitcast(FP8X4), scales=y_sc[:, g, part],
-                    in_=y_bf[:].rearrange("p c t -> p (c t)"),
-                )
-                nc.sync.dma_start(words_of(out_1, g)[:, part], y_w[:].bitcast(I32))
-
-        h_q0 = rectify(0, staging("h_bf0"))
-        we_q0 = quantise(round_weight(we_raw[0], gz9[:, 2 * PACK - 1:, :].rearrange("p t n -> p (t n)").bitcast(BF16)), "we_q0")
         wm_w = held([P, N], I32, "wm_w")
         nc.vector.tensor_copy(
             wm_w[:].rearrange("p (g t c i) -> p g c t i", g=2, t=PACK, i=4),
             wm_raw[:].rearrange("p (g c i t) -> p g c t i", g=2, t=PACK, i=4),
         )
-        slope(1, PACK - 1)
-        y_bf0 = held([P, 2, CHUNK * PACK], BF16, "y_bf0")
-        shared = y_bf0[:, 0, :]
-        we_q1 = quantise(round_weight(we_raw[1], shared), "we_q1")
-        h_q1 = rectify(1, shared)
-        y00 = second_stage(0, 0, h_q0, we_q0, wm_w)
-        y01 = second_stage(0, 1, h_q0, we_q1, wm_w)
-        y10 = second_stage(1, 0, h_q1, we_q0, wm_w)
-        y11 = second_stage(1, 1, h_q1, we_q1, wm_w)
-        for c, y in enumerate((y00, y10)):
+        for c in range(2):
+            slope(c, PACK - 1)
+
+        h_bf0 = rectify(0, staging("h_bf0"))
+        shared = held([P, PASS * PACK], BF16, "shared")[:]
+        we_q = [quantise(round_weight(we_raw[0], shared), "we_q0")]
+        h_q = [quantise(h_bf0, "h_q0")]
+        h_bf1 = rectify(1, shared)
+        we_q.append(quantise(round_weight(we_raw[1], staging("we_bf1")), "we_q1"))
+        h_q.append(quantise(h_bf1, "h_q1"))
+
+        y_sc = held([P, 2, S], U8, "y_sc")
+        y_rows = out_0.rearrange("(g p t) j -> g p t j", g=2, t=PACK)
+
+        def second_stage(g, first, width):
+            c, inner = divmod(first, CHUNK)
+            cols = slice(first, first + width)
+            within = slice(inner, inner + width)
+            y = big("y", [P, PACK, width], F32)
+            for t in range(PACK):
+                ms = slice(t * P, (t + 1) * P)
+                e = bank("e", 0, width)
+                nc.tensor.matmul_mx(
+                    out=e[:], lhsT=we_q[g][0][:, ms].bitcast(FP8X4), lhsT_scale=we_q[g][1][:, ms],
+                    rhs=h_q[c][0][:, within].bitcast(FP8X4), rhs_scale=h_q[c][1][:, within], start=True, stop=True,
+                )
+                m = bank("m", 1, width)
+                nc.tensor.matmul_mx(
+                    out=m[:], lhsT=wm_w[:, g * PASS + t * P:g * PASS + (t + 1) * P].bitcast(FP8X4),
+                    lhsT_scale=w_sc[4 + 4 * g:, ms],
+                    rhs=v2_w[:, cols].bitcast(FP8X4), rhs_scale=v2_sc[:, cols], start=True, stop=True,
+                )
+                nc.scalar.activation(y[:, t, :], e[:], SIGMOID, bias=bias[:, g, t:t + 1])
+                nc.vector.tensor_tensor(y[:, t, :], m[:], y[:, t, :], MULT)
+                if t % 2:
+                    nc.sync.dma_start(y_rows[g][:, t - 1:t + 1, cols], y[:, t - 1:t + 1, :])
+            return y
+
+        def round_on_gpsimd(y_bf, y):
             nc.gpsimd.tensor_scalar(
-                y_bf0[:, c, :].rearrange("p (c t) -> p c t", t=PACK), y[:].rearrange("p t c -> p c t"),
-                1.0, 0.0, MULT, ADD,
+                y_bf.rearrange("p (c t) -> p c t", t=PACK), y.rearrange("p t c -> p c t"), 1.0, -0.0, MULT, ADD,
             )
-        y_w0 = held([P, S], U32, "y_w0")
-        nc.vector.quantize_mx(
-            out=y_w0[:].bitcast(FP8X4), scales=y_sc[:, 0, :], in_=y_bf0[:].rearrange("p c n -> p (c n)"),
-        )
-        nc.sync.dma_start(words_of(out_1, 0), y_w0[:].bitcast(I32))
-        planes(0, 1, y01, [nc.scalar.copy])
-        planes(1, 1, y11, [nc.scalar.copy, nc.scalar.copy])
+
+        def round_on_scalar(y_bf, y):
+            nc.scalar.copy(
+                y_bf.rearrange("p (c i t) -> p c t i", i=2, t=PACK), y.rearrange("p t (c i) -> p c t i", i=2),
+            )
+
+        half = CHUNK // 2
+        units = [
+            (0, 0, CHUNK, [round_on_gpsimd, round_on_gpsimd]),
+            (1, 0, CHUNK, [round_on_gpsimd, round_on_gpsimd]),
+            (0, CHUNK, CHUNK, [round_on_gpsimd, round_on_scalar]),
+            (1, CHUNK, half, [round_on_scalar]),
+            (1, CHUNK + half, half, [round_on_scalar]),
+        ]
+        ys = [second_stage(g, first, width) for g, first, width, rounders in units]
+        staged = []
+        for u, (g, first, width, rounders) in enumerate(units):
+            y_bf = held([P, width * PACK], BF16, "y_bf%d" % u)
+            for k, rounder in enumerate(rounders):
+                rounder(y_bf[:, k * half * PACK:(k + 1) * half * PACK], ys[u][:, :, k * half:(k + 1) * half])
+            staged.append(y_bf)
+        for u, (g, first, width, rounders) in enumerate(units):
+            y_w = held([P, width], U32, "y_w%d" % u)
+            nc.vector.quantize_mx(out=y_w[:].bitcast(FP8X4), scales=y_sc[:, g, first:first + width], in_=staged[u][:])
+            nc.sync.dma_start(words_of(out_1, g)[:, first:first + width], y_w[:].bitcast(I32))
         for q in range(4):
             nc.scalar.dma_start(
                 out_2[:, 4 * q:4 * q + 4, :].bitcast(I32).rearrange("g r n -> r g n"),

@@ -47,12 +47,15 @@ def tile_list_citation_edge_gate_kernel(
         w_sc_raw = held([P, PASS], U8, "w_sc_raw")
         nc.vector.memset(tab_sc[:].bitcast(I32), 0)
         nc.vector.memset(tab2_sc[:].bitcast(I32), 0)
-        nc.gpsimd.memset(w_sc_raw[:].bitcast(I32), 0)
+        nc.vector.memset(w_sc_raw[:].bitcast(I32), 0)
 
         def big(name, shape, dtype):
             return work.tile(shape, dtype, name=name, tag="big", bufs=6, align_bytes=64)
 
-        tab_w = [big("tab_w%d" % a, [P, T], I32) for a in range(2)]
+        tab_w = [
+            work.tile([P, T], I32, name="tab_w0", tag="tab_w0", bufs=1, align_bytes=64),
+            big("tab_w1", [P, T], I32),
+        ]
         tab2_w = held([P, T2], I32, "tab2_w")
         g_win = [held([P, T], F32, "g_win%d" % t) for t in range(PACK)]
         wa_raw = [big("wa_raw%d" % a, [P, PACK, PASS], F32) for a in range(2)]
@@ -71,22 +74,24 @@ def tile_list_citation_edge_gate_kernel(
         for u in range(2):
             nc.sync.dma_start(tab_w[1][:, u * half:(u + 1) * half], words_of(tab_words, 1)[:, u * half:(u + 1) * half])
         for q in range(4):
-            nc.sync.dma_start(tab_sc[32 * q:32 * q + 8, :].bitcast(I32), tab_scales[:, 4 * q:4 * q + 4, :].bitcast(I32))
+            nc.gpsimd.dma_start(
+                tab_sc[32 * q + 4:32 * q + 12, :].bitcast(I32), tab_scales[:, 4 * q:4 * q + 4, :].bitcast(I32),
+            )
         wa_rows = wa.rearrange("(a p j) r -> a p j r", a=2, j=PACK)
         g_rows = gT.rearrange("(p t) c -> t p c", t=PACK)
         we_rows = we.rearrange("(p j) (g n) -> g p j n", j=PACK, g=2)
-        nc.sync.dma_start(wa_raw[0][:], wa_rows[0])
         for r in range(4):
             nc.sync.dma_start(tab2_sc[r:P:32, :].bitcast(I32), tab2_scales[0, r:16:4, :].bitcast(I32))
-        nc.sync.dma_start(wa_raw[1][:], wa_rows[1])
+        nc.sync.dma_start(wa_raw[0][:], wa_rows[0])
         for r in range(4):
             nc.sync.dma_start(w_sc_raw[r:P:32, :].bitcast(I32), wb_scales[0, r:16:4, :].bitcast(I32))
-        nc.sync.dma_start(tab2_w[:, :T], words_of(tab2_words, 0)[:, :T])
+        nc.sync.dma_start(wa_raw[1][:], wa_rows[1])
         for q in range(4):
-            nc.gpsimd.dma_start(
+            nc.sync.dma_start(
                 w_sc_raw[32 * q + 4:32 * q + 12, :].bitcast(I32),
                 wm_scales[0, 4 * q:4 * q + 4, :].bitcast(I32).rearrange("r (g n) -> g r n", g=2),
             )
+        nc.sync.dma_start(tab2_w[:, :T], words_of(tab2_words, 0)[:, :T])
         nc.sync.dma_start(tab2_w[:, T:], words_of(tab2_words, 0)[:, T:])
         for t in range(PACK - 1):
             nc.sync.dma_start(g_win[t][:], g_rows[t])
@@ -104,7 +109,7 @@ def tile_list_citation_edge_gate_kernel(
             wb_raw[:].bitcast(U16).rearrange("p (c i t) -> p c t i", t=PACK, i=8),
         )
         v_w = [held([P, S], U32, "v_w%d" % a) for a in range(2)]
-        v_sc = held([P, S], U8, "v_sc")
+        v_sc = work.tile([P, S], U8, name="v_sc", tag="tab_w0", bufs=1, align_bytes=64)
         v2_w = held([P, S], U32, "v2_w")
         v2_sc = held([P, S], U8, "v2_sc")
         for a in range(2):
@@ -155,7 +160,7 @@ def tile_list_citation_edge_gate_kernel(
                     ms = slice(t * P, (t + 1) * P)
                     nc.tensor.matmul_mx(
                         out=z[c][t][:], lhsT=wa_q[a][0][:, ms].bitcast(FP8X4), lhsT_scale=wa_q[a][1][:, ms],
-                        rhs=v_w[a][:, cols].bitcast(FP8X4), rhs_scale=v_sc[4 * a:, cols],
+                        rhs=v_w[a][:, cols].bitcast(FP8X4), rhs_scale=v_sc[4 + 4 * a:, cols],
                         start=(a == 0), stop=False,
                     )
         for t in range(PACK):
@@ -201,12 +206,11 @@ def tile_list_citation_edge_gate_kernel(
         h_q = [quantise(h_bf0, "h_q0")]
         h_bf1 = rectify(1, shared)
         we_q.append(quantise(round_weight(we_raw[1], staging("we_bf1")), "we_q1"))
-        h_q.append(quantise(h_bf1, "h_q1"))
 
         y_sc = held([P, 2, S], U8, "y_sc")
         y_rows = out_0.rearrange("(g p t) j -> g p t j", g=2, t=PACK)
 
-        def second_stage(g, first, width):
+        def second_stage(g, first, width, rows):
             c, inner = divmod(first, CHUNK)
             cols = slice(first, first + width)
             within = slice(inner, inner + width)
@@ -226,8 +230,8 @@ def tile_list_citation_edge_gate_kernel(
                 )
                 nc.scalar.activation(y[:, t, :], e[:], SIGMOID, bias=bias[:, g, t:t + 1])
                 nc.vector.tensor_tensor(y[:, t, :], m[:], y[:, t, :], MULT)
-                if t % 2:
-                    nc.sync.dma_start(y_rows[g][:, t - 1:t + 1, cols], y[:, t - 1:t + 1, :])
+                if (t + 1) % rows == 0:
+                    nc.sync.dma_start(y_rows[g][:, t + 1 - rows:t + 1, cols], y[:, t + 1 - rows:t + 1, :])
             return y
 
         def round_on_gpsimd(y_bf, y):
@@ -248,7 +252,9 @@ def tile_list_citation_edge_gate_kernel(
             (1, CHUNK, half, [round_on_scalar]),
             (1, CHUNK + half, half, [round_on_scalar]),
         ]
-        ys = [second_stage(g, first, width) for g, first, width, rounders in units]
+        ys = [second_stage(0, 0, CHUNK, 1)]
+        h_q.append(quantise(h_bf1, "h_q1"))
+        ys.extend(second_stage(g, first, width, 2) for g, first, width, rounders in units[1:])
         staged = []
         for u, (g, first, width, rounders) in enumerate(units):
             y_bf = held([P, width * PACK], BF16, "y_bf%d" % u)

@@ -43,7 +43,7 @@ def tile_list_citation_edge_gate_kernel(
         idx = keep.tile([P, S // 16], U16, name="idx")
         idx2 = keep.tile([P, S // 16], U16, name="idx2")
         tab_sc = held([P, T], U8, "tab_sc")
-        tab2_sc = held([P, T2], U8, "tab2_sc")
+        tab2_sc = work.tile([P, T2], U8, name="tab2_sc", tag="tab2_sc", bufs=1, align_bytes=64)
         w_sc_raw = held([P, PASS], U8, "w_sc_raw")
         nc.vector.memset(tab_sc[:].bitcast(I32), 0)
         nc.vector.memset(tab2_sc[:].bitcast(I32), 0)
@@ -52,10 +52,7 @@ def tile_list_citation_edge_gate_kernel(
         def big(name, shape, dtype):
             return work.tile(shape, dtype, name=name, tag="big", bufs=6, align_bytes=64)
 
-        tab_w = [
-            work.tile([P, T], I32, name="tab_w0", tag="tab_w0", bufs=1, align_bytes=64),
-            big("tab_w1", [P, T], I32),
-        ]
+        tab_w = [big("tab_w%d" % a, [P, T], I32) for a in range(2)]
         tab2_w = held([P, T2], I32, "tab2_w")
         g_win = [held([P, T], F32, "g_win%d" % t) for t in range(PACK)]
         wa_raw = [big("wa_raw%d" % a, [P, PACK, PASS], F32) for a in range(2)]
@@ -109,13 +106,13 @@ def tile_list_citation_edge_gate_kernel(
             wb_raw[:].bitcast(U16).rearrange("p (c i t) -> p c t i", t=PACK, i=8),
         )
         v_w = [held([P, S], U32, "v_w%d" % a) for a in range(2)]
-        v_sc = work.tile([P, S], U8, name="v_sc", tag="tab_w0", bufs=1, align_bytes=64)
+        v_sc = work.tile([P, S], U8, name="v_sc", tag="tab2_sc", bufs=1, align_bytes=64)
         v2_w = held([P, S], U32, "v2_w")
         v2_sc = held([P, S], U8, "v2_sc")
         for a in range(2):
             nc.vector.tensor_copy(v_w[a][:], tab_w[a][:].bitcast(U32).indirect(idx[:]))
-        nc.vector.tensor_copy(v_sc[:], tab_sc[:].indirect(idx[:]))
         nc.vector.tensor_copy(v2_sc[:], tab2_sc[:].indirect(idx2[:]))
+        nc.vector.tensor_copy(v_sc[:], tab_sc[:].indirect(idx[:]))
 
         def staging(name):
             return work.tile([P, PASS * PACK], BF16, name=name, tag="staged", bufs=3, align_bytes=64)[:]

@@ -43,11 +43,11 @@ def tile_list_citation_edge_gate_kernel(
         idx = keep.tile([P, S // 16], U16, name="idx")
         idx2 = keep.tile([P, S // 16], U16, name="idx2")
         tab_sc = held([P, T], U8, "tab_sc")
-        tab2_sc = work.tile([P, T2], U8, name="tab2_sc", tag="tab2_sc", bufs=1, align_bytes=64)
+        tab2_sc = held([P, T2], U8, "tab2_sc")
         w_sc_raw = held([P, PASS], U8, "w_sc_raw")
-        nc.vector.memset(tab_sc[:].bitcast(I32), 0)
+        nc.gpsimd.memset(tab_sc[:].bitcast(I32), 0)
         nc.vector.memset(tab2_sc[:].bitcast(I32), 0)
-        nc.vector.memset(w_sc_raw[:].bitcast(I32), 0)
+        nc.gpsimd.memset(w_sc_raw[:].bitcast(I32), 0)
 
         def big(name, shape, dtype):
             return work.tile(shape, dtype, name=name, tag="big", bufs=6, align_bytes=64)
@@ -61,35 +61,31 @@ def tile_list_citation_edge_gate_kernel(
         wm_raw = held([P, N], I32, "wm_raw")
         bias = held([P, 2, PACK], F32, "bias")
 
-        half = T // 2
-        nc.sync.dma_start(idx[:], offs)
-        nc.sync.dma_start(wb_raw[:].bitcast(I32), wb_words[0].bitcast(I32))
-        for u in range(2):
-            nc.sync.dma_start(tab_w[0][:, u * half:(u + 1) * half], words_of(tab_words, 0)[:, u * half:(u + 1) * half])
-        nc.sync.dma_start(idx2[:], offs2)
-        nc.sync.dma_start(bias[:], be.rearrange("(g p t) -> p g t", g=2, t=PACK))
-        for u in range(2):
-            nc.sync.dma_start(tab_w[1][:, u * half:(u + 1) * half], words_of(tab_words, 1)[:, u * half:(u + 1) * half])
-        for q in range(4):
-            nc.gpsimd.dma_start(
-                tab_sc[32 * q + 4:32 * q + 12, :].bitcast(I32), tab_scales[:, 4 * q:4 * q + 4, :].bitcast(I32),
-            )
         wa_rows = wa.rearrange("(a p j) r -> a p j r", a=2, j=PACK)
         g_rows = gT.rearrange("(p t) c -> t p c", t=PACK)
         we_rows = we.rearrange("(p j) (g n) -> g p j n", j=PACK, g=2)
-        for r in range(4):
-            nc.sync.dma_start(tab2_sc[r:P:32, :].bitcast(I32), tab2_scales[0, r:16:4, :].bitcast(I32))
-        nc.sync.dma_start(wa_raw[0][:], wa_rows[0])
-        for r in range(4):
-            nc.sync.dma_start(w_sc_raw[r:P:32, :].bitcast(I32), wb_scales[0, r:16:4, :].bitcast(I32))
-        nc.sync.dma_start(wa_raw[1][:], wa_rows[1])
+        nc.sync.dma_start(idx[:], offs)
         for q in range(4):
             nc.sync.dma_start(
+                tab_sc[32 * q + 4:32 * q + 12, :].bitcast(I32), tab_scales[:, 4 * q:4 * q + 4, :].bitcast(I32),
+            )
+        nc.sync.dma_start(tab_w[0][:], words_of(tab_words, 0))
+        nc.sync.dma_start(bias[:], be.rearrange("(g p t) -> p g t", g=2, t=PACK))
+        nc.sync.dma_start(wa_raw[0][:], wa_rows[0])
+        nc.sync.dma_start(tab_w[1][:], words_of(tab_words, 1))
+        nc.sync.dma_start(wb_raw[:].bitcast(I32), wb_words[0].bitcast(I32))
+        nc.sync.dma_start(idx2[:], offs2)
+        for r in range(4):
+            nc.sync.dma_start(tab2_sc[r:P:32, :].bitcast(I32), tab2_scales[0, r:16:4, :].bitcast(I32))
+        nc.sync.dma_start(wa_raw[1][:], wa_rows[1])
+        for r in range(4):
+            nc.sync.dma_start(w_sc_raw[r:P:32, :].bitcast(I32), wb_scales[0, r:16:4, :].bitcast(I32))
+        for q in range(4):
+            nc.gpsimd.dma_start(
                 w_sc_raw[32 * q + 4:32 * q + 12, :].bitcast(I32),
                 wm_scales[0, 4 * q:4 * q + 4, :].bitcast(I32).rearrange("r (g n) -> g r n", g=2),
             )
-        nc.sync.dma_start(tab2_w[:, :T], words_of(tab2_words, 0)[:, :T])
-        nc.sync.dma_start(tab2_w[:, T:], words_of(tab2_words, 0)[:, T:])
+        nc.sync.dma_start(tab2_w[:], words_of(tab2_words, 0))
         for t in range(PACK - 1):
             nc.sync.dma_start(g_win[t][:], g_rows[t])
         nc.sync.dma_start(wm_raw[:], words_of(wm_words, 0))
@@ -106,13 +102,13 @@ def tile_list_citation_edge_gate_kernel(
             wb_raw[:].bitcast(U16).rearrange("p (c i t) -> p c t i", t=PACK, i=8),
         )
         v_w = [held([P, S], U32, "v_w%d" % a) for a in range(2)]
-        v_sc = work.tile([P, S], U8, name="v_sc", tag="tab2_sc", bufs=1, align_bytes=64)
+        v_sc = held([P, S], U8, "v_sc")
         v2_w = held([P, S], U32, "v2_w")
         v2_sc = held([P, S], U8, "v2_sc")
+        nc.vector.tensor_copy(v_sc[:], tab_sc[:].indirect(idx[:]))
         for a in range(2):
             nc.vector.tensor_copy(v_w[a][:], tab_w[a][:].bitcast(U32).indirect(idx[:]))
         nc.vector.tensor_copy(v2_sc[:], tab2_sc[:].indirect(idx2[:]))
-        nc.vector.tensor_copy(v_sc[:], tab_sc[:].indirect(idx[:]))
 
         def staging(name):
             return work.tile([P, PASS * PACK], BF16, name=name, tag="staged", bufs=3, align_bytes=64)[:]

@@ -45,14 +45,18 @@ def tile_list_citation_edge_gate_kernel(
         tab_sc = held([P, T], U8, "tab_sc")
         tab2_sc = held([P, T2], U8, "tab2_sc")
         w_sc_raw = held([P, PASS], U8, "w_sc_raw")
-        nc.gpsimd.memset(tab_sc[:].bitcast(I32), 0)
-        nc.vector.memset(tab2_sc[:].bitcast(I32), 0)
-        nc.gpsimd.memset(w_sc_raw[:].bitcast(I32), 0)
+        nc.gpsimd.memset(tab2_sc[:, :T].bitcast(I32), 0)
+        nc.vector.memset(tab2_sc[:, T:].bitcast(I32), 0)
+        nc.vector.memset(tab_sc[:].bitcast(I32), 0)
+        nc.vector.memset(w_sc_raw[:].bitcast(I32), 0)
 
         def big(name, shape, dtype):
             return work.tile(shape, dtype, name=name, tag="big", bufs=6, align_bytes=64)
 
-        tab_w = [big("tab_w%d" % a, [P, T], I32) for a in range(2)]
+        tab_w = [
+            work.tile([P, T], I32, name="tab_w0", tag="tab_w0", bufs=1, align_bytes=64),
+            big("tab_w1", [P, T], I32),
+        ]
         tab2_w = held([P, T2], I32, "tab2_w")
         g_win = [held([P, T], F32, "g_win%d" % t) for t in range(PACK)]
         wa_raw = [big("wa_raw%d" % a, [P, PACK, PASS], F32) for a in range(2)]
@@ -64,24 +68,24 @@ def tile_list_citation_edge_gate_kernel(
         wa_rows = wa.rearrange("(a p j) r -> a p j r", a=2, j=PACK)
         g_rows = gT.rearrange("(p t) c -> t p c", t=PACK)
         we_rows = we.rearrange("(p j) (g n) -> g p j n", j=PACK, g=2)
-        nc.sync.dma_start(idx[:], offs)
+        nc.sync.dma_start(idx2[:], offs2)
+        for r in range(4):
+            nc.sync.dma_start(tab2_sc[r:P:32, :].bitcast(I32), tab2_scales[0, r:16:4, :].bitcast(I32))
         for q in range(4):
-            nc.sync.dma_start(
+            nc.gpsimd.dma_start(
                 tab_sc[32 * q + 4:32 * q + 12, :].bitcast(I32), tab_scales[:, 4 * q:4 * q + 4, :].bitcast(I32),
             )
+        nc.sync.dma_start(idx[:], offs)
         nc.sync.dma_start(tab_w[0][:], words_of(tab_words, 0))
         nc.sync.dma_start(bias[:], be.rearrange("(g p t) -> p g t", g=2, t=PACK))
         nc.sync.dma_start(wa_raw[0][:], wa_rows[0])
         nc.sync.dma_start(tab_w[1][:], words_of(tab_words, 1))
         nc.sync.dma_start(wb_raw[:].bitcast(I32), wb_words[0].bitcast(I32))
-        nc.sync.dma_start(idx2[:], offs2)
-        for r in range(4):
-            nc.sync.dma_start(tab2_sc[r:P:32, :].bitcast(I32), tab2_scales[0, r:16:4, :].bitcast(I32))
-        nc.sync.dma_start(wa_raw[1][:], wa_rows[1])
         for r in range(4):
             nc.sync.dma_start(w_sc_raw[r:P:32, :].bitcast(I32), wb_scales[0, r:16:4, :].bitcast(I32))
+        nc.sync.dma_start(wa_raw[1][:], wa_rows[1])
         for q in range(4):
-            nc.gpsimd.dma_start(
+            nc.sync.dma_start(
                 w_sc_raw[32 * q + 4:32 * q + 12, :].bitcast(I32),
                 wm_scales[0, 4 * q:4 * q + 4, :].bitcast(I32).rearrange("r (g n) -> g r n", g=2),
             )
@@ -102,13 +106,13 @@ def tile_list_citation_edge_gate_kernel(
             wb_raw[:].bitcast(U16).rearrange("p (c i t) -> p c t i", t=PACK, i=8),
         )
         v_w = [held([P, S], U32, "v_w%d" % a) for a in range(2)]
-        v_sc = held([P, S], U8, "v_sc")
+        v_sc = work.tile([P, S], U8, name="v_sc", tag="tab_w0", bufs=1, align_bytes=64)
         v2_w = held([P, S], U32, "v2_w")
         v2_sc = held([P, S], U8, "v2_sc")
-        nc.vector.tensor_copy(v_sc[:], tab_sc[:].indirect(idx[:]))
-        for a in range(2):
-            nc.vector.tensor_copy(v_w[a][:], tab_w[a][:].bitcast(U32).indirect(idx[:]))
         nc.vector.tensor_copy(v2_sc[:], tab2_sc[:].indirect(idx2[:]))
+        nc.vector.tensor_copy(v_w[0][:], tab_w[0][:].bitcast(U32).indirect(idx[:]))
+        nc.vector.tensor_copy(v_sc[:], tab_sc[:].indirect(idx[:]))
+        nc.vector.tensor_copy(v_w[1][:], tab_w[1][:].bitcast(U32).indirect(idx[:]))
 
         def staging(name):
             return work.tile([P, PASS * PACK], BF16, name=name, tag="staged", bufs=3, align_bytes=64)[:]
@@ -203,12 +207,11 @@ def tile_list_citation_edge_gate_kernel(
         y_sc = held([P, 2, S], U8, "y_sc")
         y_rows = out_0.rearrange("(g p t) j -> g p t j", g=2, t=PACK)
 
-        def second_stage(g, first, width, rows):
+        def second_stage(y, g, first, width, slices, rows):
             c, inner = divmod(first, CHUNK)
             cols = slice(first, first + width)
             within = slice(inner, inner + width)
-            y = big("y", [P, PACK, width], F32)
-            for t in range(PACK):
+            for t in slices:
                 ms = slice(t * P, (t + 1) * P)
                 e = bank("e", 0, width)
                 nc.tensor.matmul_mx(
@@ -225,7 +228,6 @@ def tile_list_citation_edge_gate_kernel(
                 nc.vector.tensor_tensor(y[:, t, :], m[:], y[:, t, :], MULT)
                 if (t + 1) % rows == 0:
                     nc.sync.dma_start(y_rows[g][:, t + 1 - rows:t + 1, cols], y[:, t + 1 - rows:t + 1, :])
-            return y
 
         def round_on_gpsimd(y_bf, y):
             nc.gpsimd.tensor_scalar(
@@ -239,27 +241,30 @@ def tile_list_citation_edge_gate_kernel(
 
         half = CHUNK // 2
         units = [
-            (0, 0, CHUNK, [round_on_gpsimd, round_on_gpsimd]),
-            (1, 0, CHUNK, [round_on_gpsimd, round_on_gpsimd]),
-            (0, CHUNK, CHUNK, [round_on_gpsimd, round_on_scalar]),
-            (1, CHUNK, half, [round_on_scalar]),
-            (1, CHUNK + half, half, [round_on_scalar]),
+            (0, 0, CHUNK, [(round_on_gpsimd, 0, half), (round_on_gpsimd, half, CHUNK)]),
+            (1, 0, CHUNK, [(round_on_gpsimd, 0, half), (round_on_gpsimd, half, CHUNK)]),
+            (0, CHUNK, CHUNK, [(round_on_gpsimd, 0, half // 2), (round_on_scalar, half // 2, CHUNK)]),
+            (1, CHUNK, half, [(round_on_scalar, 0, half)]),
+            (1, CHUNK + half, half, [(round_on_scalar, 0, half)]),
         ]
-        ys = [second_stage(0, 0, CHUNK, 1)]
+        ys = [big("y", [P, PACK, width], F32) for g, first, width, shares in units]
+        second_stage(ys[0], 0, 0, CHUNK, range(2), 1)
         h_q.append(quantise(h_bf1, "h_q1"))
-        ys.extend(second_stage(g, first, width, 2) for g, first, width, rounders in units[1:])
+        second_stage(ys[0], 0, 0, CHUNK, range(2, PACK), 1)
+        for u, (g, first, width, shares) in enumerate(units[1:]):
+            second_stage(ys[u + 1], g, first, width, range(PACK), 2)
         staged = []
-        for u, (g, first, width, rounders) in enumerate(units):
+        for u, (g, first, width, shares) in enumerate(units):
             y_bf = held([P, width * PACK], BF16, "y_bf%d" % u)
-            for k, rounder in enumerate(rounders):
-                rounder(y_bf[:, k * half * PACK:(k + 1) * half * PACK], ys[u][:, :, k * half:(k + 1) * half])
+            for rounder, lo, hi in shares:
+                rounder(y_bf[:, lo * PACK:hi * PACK], ys[u][:, :, lo:hi])
             staged.append(y_bf)
-        for u, (g, first, width, rounders) in enumerate(units):
+        for u, (g, first, width, shares) in enumerate(units):
             y_w = held([P, width], U32, "y_w%d" % u)
             nc.vector.quantize_mx(out=y_w[:].bitcast(FP8X4), scales=y_sc[:, g, first:first + width], in_=staged[u][:])
             nc.sync.dma_start(words_of(out_1, g)[:, first:first + width], y_w[:].bitcast(I32))
-        for q in range(4):
+        for r in range(4):
             nc.scalar.dma_start(
-                out_2[:, 4 * q:4 * q + 4, :].bitcast(I32).rearrange("g r n -> r g n"),
-                y_sc[32 * q:32 * q + 4, :, :].bitcast(I32),
+                out_2[:, r:16:4, :].bitcast(I32).rearrange("g q n -> q g n"),
+                y_sc[r:P:32, :, :].bitcast(I32),
             )

@@ -69,36 +69,35 @@ def tile_list_citation_edge_gate_kernel(
         g_rows = gT.rearrange("(p t) c -> t p c", t=PACK)
         we_rows = we.rearrange("(p j) (g n) -> g p j n", j=PACK, g=2)
         nc.sync.dma_start(idx2[:], offs2)
+        nc.sync.dma_start(idx[:], offs)
+        nc.sync.dma_start(wb_raw[:].bitcast(I32), wb_words[0].bitcast(I32))
         for r in range(4):
             nc.sync.dma_start(tab2_sc[r:P:32, :].bitcast(I32), tab2_scales[0, r:16:4, :].bitcast(I32))
         for q in range(4):
             nc.gpsimd.dma_start(
                 tab_sc[32 * q + 4:32 * q + 12, :].bitcast(I32), tab_scales[:, 4 * q:4 * q + 4, :].bitcast(I32),
             )
-        nc.sync.dma_start(idx[:], offs)
-        nc.sync.dma_start(tab_w[0][:], words_of(tab_words, 0))
-        nc.sync.dma_start(bias[:], be.rearrange("(g p t) -> p g t", g=2, t=PACK))
-        nc.sync.dma_start(wa_raw[0][:], wa_rows[0])
-        nc.sync.dma_start(tab_w[1][:], words_of(tab_words, 1))
-        nc.sync.dma_start(wb_raw[:].bitcast(I32), wb_words[0].bitcast(I32))
         for r in range(4):
-            nc.sync.dma_start(w_sc_raw[r:P:32, :].bitcast(I32), wb_scales[0, r:16:4, :].bitcast(I32))
-        nc.sync.dma_start(wa_raw[1][:], wa_rows[1])
+            nc.gpsimd.dma_start(w_sc_raw[r:P:32, :].bitcast(I32), wb_scales[0, r:16:4, :].bitcast(I32))
         for q in range(4):
-            nc.sync.dma_start(
+            nc.gpsimd.dma_start(
                 w_sc_raw[32 * q + 4:32 * q + 12, :].bitcast(I32),
                 wm_scales[0, 4 * q:4 * q + 4, :].bitcast(I32).rearrange("r (g n) -> g r n", g=2),
             )
+        nc.sync.dma_start(tab_w[0][:], words_of(tab_words, 0))
+        nc.sync.dma_start(wa_raw[0][:], wa_rows[0])
+        nc.sync.dma_start(wa_raw[1][:], wa_rows[1])
+        nc.sync.dma_start(tab_w[1][:], words_of(tab_words, 1))
         nc.sync.dma_start(tab2_w[:], words_of(tab2_words, 0))
-        for t in range(PACK - 1):
-            nc.sync.dma_start(g_win[t][:], g_rows[t])
         nc.sync.dma_start(wm_raw[:], words_of(wm_words, 0))
-        nc.sync.dma_start(g_win[PACK - 1][:], g_rows[PACK - 1])
+        for t in range(PACK):
+            nc.sync.dma_start(g_win[t][:], g_rows[t])
+        nc.sync.dma_start(bias[:], be.rearrange("(g p t) -> p g t", g=2, t=PACK))
         nc.sync.dma_start(we_raw[0][:], we_rows[0])
         nc.sync.dma_start(we_raw[1][:], we_rows[1])
 
         warm = held([P, 1], F32, "warm")
-        nc.scalar.activation(warm[:], bias[:, 0, 0:1], SIGMOID)
+        nc.scalar.activation(warm[:], wa_raw[0][:, 0, 0:1], SIGMOID)
 
         wb_w = held([P, 2 * H], U8, "wb_w")
         nc.vector.tensor_copy(
@@ -131,17 +130,27 @@ def tile_list_citation_edge_gate_kernel(
             nc.vector.quantize_mx(out=codes[:].bitcast(FP8X4), scales=scales[:], in_=staged)
             return codes, scales
 
-        w_sc = held([P, PASS], U8, "w_sc")
+        wa_bf1 = work.tile([P, PASS * PACK], BF16, name="wa_bf1", tag="wa_bf1", bufs=1, align_bytes=64)
+        wa_q = [
+            quantise(round_weight(wa_raw[0], staging("wa_bf0")), "wa_q0"),
+            quantise(round_weight(wa_raw[1], wa_bf1[:]), "wa_q1"),
+        ]
+        w_sc = work.tile([P, PASS], U8, name="w_sc", tag="wa_bf1", bufs=1, align_bytes=64)
         nc.vector.tensor_copy(
             w_sc[:].rearrange("p (t c i) -> p c t i", t=PACK, i=16),
             w_sc_raw[:].rearrange("p (c i t) -> p c t i", t=PACK, i=16),
         )
-        wa_q = [quantise(round_weight(wa_raw[a], staging("wa_bf%d" % a)), "wa_q%d" % a) for a in range(2)]
         for c in range(2):
             nc.vector.tensor_copy(
                 v2_w[:, c * CHUNK:(c + 1) * CHUNK],
                 tab2_w[:].bitcast(U32).indirect(idx2[:, c * CHUNK // 16:(c + 1) * CHUNK // 16]),
             )
+
+        wm_w = held([P, N], I32, "wm_w")
+        nc.vector.tensor_copy(
+            wm_w[:].rearrange("p (g t c i) -> p g c t i", g=2, t=PACK, i=4),
+            wm_raw[:].rearrange("p (g c i t) -> p g c t i", g=2, t=PACK, i=4),
+        )
 
         z_sb = [held([P, PACK, CHUNK], F32, "z_sb%d" % c) for c in range(2)]
         gz = [held([P, PACK, CHUNK], F32, "gz%d" % c) for c in range(2)]
@@ -186,16 +195,9 @@ def tile_list_citation_edge_gate_kernel(
             )
             return h_bf
 
-        for t in range(PACK - 1):
+        for t in range(PACK):
             for c in range(2):
                 slope(c, t)
-        wm_w = held([P, N], I32, "wm_w")
-        nc.vector.tensor_copy(
-            wm_w[:].rearrange("p (g t c i) -> p g c t i", g=2, t=PACK, i=4),
-            wm_raw[:].rearrange("p (g c i t) -> p g c t i", g=2, t=PACK, i=4),
-        )
-        for c in range(2):
-            slope(c, PACK - 1)
 
         h_bf0 = rectify(0, staging("h_bf0"))
         shared = held([P, PASS * PACK], BF16, "shared")[:]

@@ -32,6 +32,7 @@ def tile_list_citation_edge_gate_kernel(
     with ExitStack() as ctx:
         keep = ctx.enter_context(tc.tile_pool(name="keep", bufs=1))
         work = ctx.enter_context(tc.tile_pool(name="work", bufs=1))
+        reused = ctx.enter_context(tc.tile_pool(name="reused", bufs=1))
         psum = ctx.enter_context(tc.psum_pool(name="psum", bufs=1))
 
         def held(shape, dtype, name):
@@ -51,7 +52,7 @@ def tile_list_citation_edge_gate_kernel(
         nc.vector.memset(w_sc_raw[:].bitcast(I32), 0)
 
         def big(name, shape, dtype):
-            return work.tile(shape, dtype, name=name, tag="big", bufs=6, align_bytes=64)
+            return work.tile(shape, dtype, name=name, tag="big", bufs=5, align_bytes=64)
 
         tab_w = [
             work.tile([P, T], I32, name="tab_w0", tag="tab_w0", bufs=1, align_bytes=64),
@@ -59,8 +60,14 @@ def tile_list_citation_edge_gate_kernel(
         ]
         tab2_w = held([P, T2], I32, "tab2_w")
         g_win = [held([P, T], F32, "g_win%d" % t) for t in range(PACK)]
-        wa_raw = [big("wa_raw%d" % a, [P, PACK, PASS], F32) for a in range(2)]
-        we_raw = [big("we_raw%d" % g, [P, PACK, PASS], F32) for g in range(2)]
+        wa_raw = [
+            big("wa_raw0", [P, PACK, PASS], F32),
+            work.tile([P, PACK, PASS], F32, name="wa_raw1", tag="wa_raw1", bufs=1, align_bytes=64),
+        ]
+        we_raw = [
+            reused.tile([P, PACK, PASS], F32, name="we_raw0", offset=0, align_bytes=64),
+            big("we_raw1", [P, PACK, PASS], F32),
+        ]
         wb_raw = held([P, 2 * H], U8, "wb_raw")
         wm_raw = held([P, N], I32, "wm_raw")
         bias = held([P, 2, PACK], F32, "bias")
@@ -124,18 +131,15 @@ def tile_list_citation_edge_gate_kernel(
                 )
             return staged
 
-        def quantise(staged, name):
+        def quantise(staged, name, scales=None):
             codes = held([P, PASS], U32, name + "_w")
-            scales = held([P, PASS], U8, name + "_sc")
+            if scales is None:
+                scales = held([P, PASS], U8, name + "_sc")
             nc.vector.quantize_mx(out=codes[:].bitcast(FP8X4), scales=scales[:], in_=staged)
             return codes, scales
 
-        wa_bf1 = work.tile([P, PASS * PACK], BF16, name="wa_bf1", tag="wa_bf1", bufs=1, align_bytes=64)
-        wa_q = [
-            quantise(round_weight(wa_raw[0], staging("wa_bf0")), "wa_q0"),
-            quantise(round_weight(wa_raw[1], wa_bf1[:]), "wa_q1"),
-        ]
-        w_sc = work.tile([P, PASS], U8, name="w_sc", tag="wa_bf1", bufs=1, align_bytes=64)
+        wa_q = [quantise(round_weight(wa_raw[a], staging("wa_bf%d" % a)), "wa_q%d" % a) for a in range(2)]
+        w_sc = work.tile([P, PASS], U8, name="w_sc", tag="wa_raw1", bufs=1, align_bytes=64)
         nc.vector.tensor_copy(
             w_sc[:].rearrange("p (t c i) -> p c t i", t=PACK, i=16),
             w_sc_raw[:].rearrange("p (c i t) -> p c t i", t=PACK, i=16),
@@ -152,8 +156,8 @@ def tile_list_citation_edge_gate_kernel(
             wm_raw[:].rearrange("p (g c i t) -> p g c t i", g=2, t=PACK, i=4),
         )
 
-        z_sb = [held([P, PACK, CHUNK], F32, "z_sb%d" % c) for c in range(2)]
-        gz = [held([P, PACK, CHUNK], F32, "gz%d" % c) for c in range(2)]
+        z_sb = held([P, PACK, S], F32, "z_sb")
+        gz = held([P, PACK, S], F32, "gz")
 
         def bank(name, c, width):
             return psum.tile([P, width], F32, name=name, tag="bank%d" % c, bufs=4)
@@ -178,32 +182,32 @@ def tile_list_citation_edge_gate_kernel(
                     rhs=v2_w[:, cols].bitcast(FP8X4), rhs_scale=v2_sc[:, cols],
                     start=False, stop=True,
                 )
-                nc.scalar.copy(z_sb[c][:, t, :], z[c][t][:])
+                nc.scalar.copy(z_sb[:, t, cols], z[c][t][:])
 
-        def slope(c, t):
+        def slope(t, lo, hi):
             nc.vector.tensor_tensor(
-                gz[c][:, t, :], g_win[t][:].indirect(idx[:, c * CHUNK // 16:(c + 1) * CHUNK // 16]),
-                z_sb[c][:, t, :], MULT,
+                gz[:, t, lo:hi], g_win[t][:].indirect(idx[:, lo // 16:hi // 16]), z_sb[:, t, lo:hi], MULT,
             )
 
         def rectify(c, h_bf):
             nc.vector.tensor_tensor(
                 h_bf.rearrange("p (c i t) -> p c t i", i=2, t=PACK),
-                z_sb[c][:].rearrange("p t (c i) -> p c t i", i=2),
-                gz[c][:].rearrange("p t (c i) -> p c t i", i=2),
+                z_sb[:, :, c * CHUNK:(c + 1) * CHUNK].rearrange("p t (c i) -> p c t i", i=2),
+                gz[:, :, c * CHUNK:(c + 1) * CHUNK].rearrange("p t (c i) -> p c t i", i=2),
                 MAX,
             )
             return h_bf
 
         for t in range(PACK):
-            for c in range(2):
-                slope(c, t)
+            width = CHUNK if t in (0, PACK - 1) else S
+            for lo in range(0, S, width):
+                slope(t, lo, lo + width)
 
         h_bf0 = rectify(0, staging("h_bf0"))
-        shared = held([P, PASS * PACK], BF16, "shared")[:]
-        we_q = [quantise(round_weight(we_raw[0], shared), "we_q0")]
-        h_q = [quantise(h_bf0, "h_q0")]
-        h_bf1 = rectify(1, shared)
+        we_q = [quantise(round_weight(we_raw[0], held([P, PASS * PACK], BF16, "we_bf0")[:]), "we_q0")]
+        h_q0_sc = reused.tile([P, PASS], U8, name="h_q0_sc", offset=2 * PASS * PACK, align_bytes=64)
+        h_q = [quantise(h_bf0, "h_q0", h_q0_sc)]
+        h_bf1 = rectify(1, reused.tile([P, PASS * PACK], BF16, name="h_bf1", offset=0, align_bytes=64)[:])
         we_q.append(quantise(round_weight(we_raw[1], staging("we_bf1")), "we_q1"))
 
         y_sc = held([P, 2, S], U8, "y_sc")

@@ -45,11 +45,13 @@ def tile_list_citation_edge_gate_kernel(
         idx2 = keep.tile([P, S // 16], U16, name="idx2")
         tab_sc = held([P, T], U8, "tab_sc")
         tab2_sc = held([P, T2], U8, "tab2_sc")
-        w_sc_raw = held([P, PASS], U8, "w_sc_raw")
+        wb_sc_raw = held([P, PASS], U8, "wb_sc_raw")
+        wm_sc_raw = held([P, PASS], U8, "wm_sc_raw")
         nc.gpsimd.memset(tab2_sc[:, :T].bitcast(I32), 0)
         nc.vector.memset(tab2_sc[:, T:].bitcast(I32), 0)
         nc.vector.memset(tab_sc[:].bitcast(I32), 0)
-        nc.vector.memset(w_sc_raw[:].bitcast(I32), 0)
+        nc.vector.memset(wb_sc_raw[:].bitcast(I32), 0)
+        nc.vector.memset(wm_sc_raw[:].bitcast(I32), 0)
 
         def big(name, shape, dtype):
             return work.tile(shape, dtype, name=name, tag="big", bufs=5, align_bytes=64)
@@ -58,7 +60,7 @@ def tile_list_citation_edge_gate_kernel(
             work.tile([P, T], I32, name="tab_w0", tag="tab_w0", bufs=1, align_bytes=64),
             big("tab_w1", [P, T], I32),
         ]
-        tab2_w = held([P, T2], I32, "tab2_w")
+        tab2_w = work.tile([P, T2], I32, name="tab2_w", tag="tab2_w", bufs=1, align_bytes=64)
         g_win = [held([P, T], F32, "g_win%d" % t) for t in range(PACK)]
         wa_raw = [
             big("wa_raw0", [P, PACK, PASS], F32),
@@ -84,14 +86,14 @@ def tile_list_citation_edge_gate_kernel(
             nc.gpsimd.dma_start(
                 tab_sc[32 * q + 4:32 * q + 12, :].bitcast(I32), tab_scales[:, 4 * q:4 * q + 4, :].bitcast(I32),
             )
-        for r in range(4):
-            nc.gpsimd.dma_start(w_sc_raw[r:P:32, :].bitcast(I32), wb_scales[0, r:16:4, :].bitcast(I32))
         for q in range(4):
             nc.gpsimd.dma_start(
-                w_sc_raw[32 * q + 4:32 * q + 12, :].bitcast(I32),
+                wm_sc_raw[32 * q:32 * q + 8, :].bitcast(I32),
                 wm_scales[0, 4 * q:4 * q + 4, :].bitcast(I32).rearrange("r (g n) -> g r n", g=2),
             )
         nc.sync.dma_start(tab_w[0][:], words_of(tab_words, 0))
+        for r in range(4):
+            nc.sync.dma_start(wb_sc_raw[r:P:32, :].bitcast(I32), wb_scales[0, r:16:4, :].bitcast(I32))
         nc.sync.dma_start(wa_raw[0][:], wa_rows[0])
         nc.sync.dma_start(wa_raw[1][:], wa_rows[1])
         nc.sync.dma_start(tab_w[1][:], words_of(tab_words, 1))
@@ -139,11 +141,15 @@ def tile_list_citation_edge_gate_kernel(
             return codes, scales
 
         wa_q = [quantise(round_weight(wa_raw[a], staging("wa_bf%d" % a)), "wa_q%d" % a) for a in range(2)]
-        w_sc = work.tile([P, PASS], U8, name="w_sc", tag="wa_raw1", bufs=1, align_bytes=64)
-        nc.vector.tensor_copy(
-            w_sc[:].rearrange("p (t c i) -> p c t i", t=PACK, i=16),
-            w_sc_raw[:].rearrange("p (c i t) -> p c t i", t=PACK, i=16),
-        )
+
+        def deal_scales(dealt, raw):
+            nc.vector.tensor_copy(
+                dealt[:].rearrange("p (t c i) -> p c t i", t=PACK, i=16),
+                raw[:].rearrange("p (c i t) -> p c t i", t=PACK, i=16),
+            )
+            return dealt
+
+        wb_sc = deal_scales(work.tile([P, PASS], U8, name="wb_sc", tag="wa_raw1", bufs=1, align_bytes=64), wb_sc_raw)
         for c in range(2):
             nc.vector.tensor_copy(
                 v2_w[:, c * CHUNK:(c + 1) * CHUNK],
@@ -155,6 +161,8 @@ def tile_list_citation_edge_gate_kernel(
             wm_w[:].rearrange("p (g t c i) -> p g c t i", g=2, t=PACK, i=4),
             wm_raw[:].rearrange("p (g c i t) -> p g c t i", g=2, t=PACK, i=4),
         )
+
+        wm_sc = deal_scales(work.tile([P, PASS], U8, name="wm_sc", tag="tab2_w", bufs=1, align_bytes=64), wm_sc_raw)
 
         z_sb = held([P, PACK, S], F32, "z_sb")
         gz = held([P, PACK, S], F32, "gz")
@@ -178,7 +186,7 @@ def tile_list_citation_edge_gate_kernel(
             for c in range(2):
                 cols = slice(c * CHUNK, (c + 1) * CHUNK)
                 nc.tensor.matmul_mx(
-                    out=z[c][t][:], lhsT=wb_w[:, 2 * t * P:2 * (t + 1) * P].bitcast(FP4X4), lhsT_scale=w_sc[:, ms],
+                    out=z[c][t][:], lhsT=wb_w[:, 2 * t * P:2 * (t + 1) * P].bitcast(FP4X4), lhsT_scale=wb_sc[:, ms],
                     rhs=v2_w[:, cols].bitcast(FP8X4), rhs_scale=v2_sc[:, cols],
                     start=False, stop=True,
                 )
@@ -227,7 +235,7 @@ def tile_list_citation_edge_gate_kernel(
                 m = bank("m", 1, width)
                 nc.tensor.matmul_mx(
                     out=m[:], lhsT=wm_w[:, g * PASS + t * P:g * PASS + (t + 1) * P].bitcast(FP8X4),
-                    lhsT_scale=w_sc[4 + 4 * g:, ms],
+                    lhsT_scale=wm_sc[4 * g:, ms],
                     rhs=v2_w[:, cols].bitcast(FP8X4), rhs_scale=v2_sc[:, cols], start=True, stop=True,
                 )
                 nc.scalar.activation(y[:, t, :], e[:], SIGMOID, bias=bias[:, g, t:t + 1])

@@ -33,6 +33,7 @@ def tile_list_citation_edge_gate_kernel(
         keep = ctx.enter_context(tc.tile_pool(name="keep", bufs=1))
         work = ctx.enter_context(tc.tile_pool(name="work", bufs=1))
         reused = ctx.enter_context(tc.tile_pool(name="reused", bufs=1))
+        early = ctx.enter_context(tc.tile_pool(name="early", bufs=1))
         psum = ctx.enter_context(tc.psum_pool(name="psum", bufs=1))
 
         def held(shape, dtype, name):
@@ -44,7 +45,7 @@ def tile_list_citation_edge_gate_kernel(
         idx = keep.tile([P, S // 16], U16, name="idx")
         idx2 = keep.tile([P, S // 16], U16, name="idx2")
         tab_sc = held([P, T], U8, "tab_sc")
-        tab2_sc = held([P, T2], U8, "tab2_sc")
+        tab2_sc = early.tile([P, T2], U8, name="tab2_sc", offset=0, align_bytes=64)
         wb_sc_raw = held([P, PASS], U8, "wb_sc_raw")
         wm_sc_raw = held([P, PASS], U8, "wm_sc_raw")
         nc.gpsimd.memset(tab2_sc[:, :T].bitcast(I32), 0)
@@ -57,7 +58,7 @@ def tile_list_citation_edge_gate_kernel(
             return work.tile(shape, dtype, name=name, tag="big", bufs=5, align_bytes=64)
 
         tab_w = [
-            work.tile([P, T], I32, name="tab_w0", tag="tab_w0", bufs=1, align_bytes=64),
+            early.tile([P, T], I32, name="tab_w0", offset=T2, align_bytes=64),
             big("tab_w1", [P, T], I32),
         ]
         tab2_w = work.tile([P, T2], I32, name="tab2_w", tag="tab2_w", bufs=1, align_bytes=64)
@@ -78,10 +79,10 @@ def tile_list_citation_edge_gate_kernel(
         g_rows = gT.rearrange("(p t) c -> t p c", t=PACK)
         we_rows = we.rearrange("(p j) (g n) -> g p j n", j=PACK, g=2)
         nc.sync.dma_start(idx2[:], offs2)
+        nc.sync.dma_start(tab_w[0][:], words_of(tab_words, 0))
         nc.sync.dma_start(idx[:], offs)
-        nc.sync.dma_start(wb_raw[:].bitcast(I32), wb_words[0].bitcast(I32))
         for r in range(4):
-            nc.sync.dma_start(tab2_sc[r:P:32, :].bitcast(I32), tab2_scales[0, r:16:4, :].bitcast(I32))
+            nc.scalar.dma_start(tab2_sc[r:P:32, :].bitcast(I32), tab2_scales[0, r:16:4, :].bitcast(I32))
         for q in range(4):
             nc.gpsimd.dma_start(
                 tab_sc[32 * q + 4:32 * q + 12, :].bitcast(I32), tab_scales[:, 4 * q:4 * q + 4, :].bitcast(I32),
@@ -91,12 +92,12 @@ def tile_list_citation_edge_gate_kernel(
                 wm_sc_raw[32 * q:32 * q + 8, :].bitcast(I32),
                 wm_scales[0, 4 * q:4 * q + 4, :].bitcast(I32).rearrange("r (g n) -> g r n", g=2),
             )
-        nc.sync.dma_start(tab_w[0][:], words_of(tab_words, 0))
-        for r in range(4):
-            nc.sync.dma_start(wb_sc_raw[r:P:32, :].bitcast(I32), wb_scales[0, r:16:4, :].bitcast(I32))
         nc.sync.dma_start(wa_raw[0][:], wa_rows[0])
         nc.sync.dma_start(wa_raw[1][:], wa_rows[1])
         nc.sync.dma_start(tab_w[1][:], words_of(tab_words, 1))
+        for r in range(4):
+            nc.sync.dma_start(wb_sc_raw[r:P:32, :].bitcast(I32), wb_scales[0, r:16:4, :].bitcast(I32))
+        nc.sync.dma_start(wb_raw[:].bitcast(I32), wb_words[0].bitcast(I32))
         nc.sync.dma_start(tab2_w[:], words_of(tab2_words, 0))
         nc.sync.dma_start(wm_raw[:], words_of(wm_words, 0))
         for t in range(PACK):
@@ -108,13 +109,8 @@ def tile_list_citation_edge_gate_kernel(
         warm = held([P, 1], F32, "warm")
         nc.scalar.activation(warm[:], wa_raw[0][:, 0, 0:1], SIGMOID)
 
-        wb_w = held([P, 2 * H], U8, "wb_w")
-        nc.vector.tensor_copy(
-            wb_w[:].bitcast(U16).rearrange("p (t c i) -> p c t i", t=PACK, i=8),
-            wb_raw[:].bitcast(U16).rearrange("p (c i t) -> p c t i", t=PACK, i=8),
-        )
         v_w = [held([P, S], U32, "v_w%d" % a) for a in range(2)]
-        v_sc = work.tile([P, S], U8, name="v_sc", tag="tab_w0", bufs=1, align_bytes=64)
+        v_sc = early.tile([P, S], U8, name="v_sc", offset=T2 - S // 2, align_bytes=64)
         v2_w = held([P, S], U32, "v2_w")
         v2_sc = held([P, S], U8, "v2_sc")
         nc.vector.tensor_copy(v2_sc[:], tab2_sc[:].indirect(idx2[:]))
@@ -141,6 +137,11 @@ def tile_list_citation_edge_gate_kernel(
             return codes, scales
 
         wa_q = [quantise(round_weight(wa_raw[a], staging("wa_bf%d" % a)), "wa_q%d" % a) for a in range(2)]
+        wb_w = held([P, 2 * H], U8, "wb_w")
+        nc.scalar.copy(
+            wb_w[:].bitcast(U16).rearrange("p (t c i) -> p c t i", t=PACK, i=8),
+            wb_raw[:].bitcast(U16).rearrange("p (c i t) -> p c t i", t=PACK, i=8),
+        )
 
         def deal_scales(dealt, raw):
             nc.vector.tensor_copy(

@@ -78,15 +78,17 @@ def tile_list_citation_edge_gate_kernel(
         wa_rows = wa.rearrange("(a p j) r -> a p j r", a=2, j=PACK)
         g_rows = gT.rearrange("(p t) c -> t p c", t=PACK)
         we_rows = we.rearrange("(p j) (g n) -> g p j n", j=PACK, g=2)
-        nc.sync.dma_start(idx2[:], offs2)
-        nc.sync.dma_start(tab_w[0][:], words_of(tab_words, 0))
         nc.sync.dma_start(idx[:], offs)
+        nc.sync.dma_start(tab_w[0][:], words_of(tab_words, 0))
+        nc.sync.dma_start(idx2[:], offs2)
         for r in range(4):
-            nc.scalar.dma_start(tab2_sc[r:P:32, :].bitcast(I32), tab2_scales[0, r:16:4, :].bitcast(I32))
+            nc.sync.dma_start(tab2_sc[r:P:32, :].bitcast(I32), tab2_scales[0, r:16:4, :].bitcast(I32))
         for q in range(4):
             nc.gpsimd.dma_start(
                 tab_sc[32 * q + 4:32 * q + 12, :].bitcast(I32), tab_scales[:, 4 * q:4 * q + 4, :].bitcast(I32),
             )
+        for r in range(4):
+            nc.gpsimd.dma_start(wb_sc_raw[r:P:32, :].bitcast(I32), wb_scales[0, r:16:4, :].bitcast(I32))
         for q in range(4):
             nc.gpsimd.dma_start(
                 wm_sc_raw[32 * q:32 * q + 8, :].bitcast(I32),
@@ -95,13 +97,12 @@ def tile_list_citation_edge_gate_kernel(
         nc.sync.dma_start(wa_raw[0][:], wa_rows[0])
         nc.sync.dma_start(wa_raw[1][:], wa_rows[1])
         nc.sync.dma_start(tab_w[1][:], words_of(tab_words, 1))
-        for r in range(4):
-            nc.sync.dma_start(wb_sc_raw[r:P:32, :].bitcast(I32), wb_scales[0, r:16:4, :].bitcast(I32))
-        nc.sync.dma_start(wb_raw[:].bitcast(I32), wb_words[0].bitcast(I32))
         nc.sync.dma_start(tab2_w[:], words_of(tab2_words, 0))
-        nc.sync.dma_start(wm_raw[:], words_of(wm_words, 0))
-        for t in range(PACK):
+        nc.sync.dma_start(wb_raw[:].bitcast(I32), wb_words[0].bitcast(I32))
+        for t in range(PACK - 1):
             nc.sync.dma_start(g_win[t][:], g_rows[t])
+        nc.sync.dma_start(wm_raw[:], words_of(wm_words, 0))
+        nc.sync.dma_start(g_win[PACK - 1][:], g_rows[PACK - 1])
         nc.sync.dma_start(bias[:], be.rearrange("(g p t) -> p g t", g=2, t=PACK))
         nc.sync.dma_start(we_raw[0][:], we_rows[0])
         nc.sync.dma_start(we_raw[1][:], we_rows[1])
@@ -109,12 +110,12 @@ def tile_list_citation_edge_gate_kernel(
         warm = held([P, 1], F32, "warm")
         nc.scalar.activation(warm[:], wa_raw[0][:, 0, 0:1], SIGMOID)
 
-        v_w = [held([P, S], U32, "v_w%d" % a) for a in range(2)]
+        v_w = [work.tile([P, S], U32, name="v_w%d" % a, tag="v_w%d" % a, bufs=1, align_bytes=64) for a in range(2)]
         v_sc = early.tile([P, S], U8, name="v_sc", offset=T2 - S // 2, align_bytes=64)
         v2_w = held([P, S], U32, "v2_w")
         v2_sc = held([P, S], U8, "v2_sc")
-        nc.vector.tensor_copy(v2_sc[:], tab2_sc[:].indirect(idx2[:]))
         nc.vector.tensor_copy(v_w[0][:], tab_w[0][:].bitcast(U32).indirect(idx[:]))
+        nc.vector.tensor_copy(v2_sc[:], tab2_sc[:].indirect(idx2[:]))
         nc.vector.tensor_copy(v_sc[:], tab_sc[:].indirect(idx[:]))
         nc.vector.tensor_copy(v_w[1][:], tab_w[1][:].bitcast(U32).indirect(idx[:]))
 
@@ -157,11 +158,6 @@ def tile_list_citation_edge_gate_kernel(
                 tab2_w[:].bitcast(U32).indirect(idx2[:, c * CHUNK // 16:(c + 1) * CHUNK // 16]),
             )
 
-        wm_w = held([P, N], I32, "wm_w")
-        nc.vector.tensor_copy(
-            wm_w[:].rearrange("p (g t c i) -> p g c t i", g=2, t=PACK, i=4),
-            wm_raw[:].rearrange("p (g c i t) -> p g c t i", g=2, t=PACK, i=4),
-        )
 
         wm_sc = deal_scales(work.tile([P, PASS], U8, name="wm_sc", tag="tab2_w", bufs=1, align_bytes=64), wm_sc_raw)
 
@@ -172,26 +168,39 @@ def tile_list_citation_edge_gate_kernel(
             return psum.tile([P, width], F32, name=name, tag="bank%d" % c, bufs=4)
 
         z = [[bank("z", c, CHUNK) for t in range(PACK)] for c in range(2)]
-        for a in range(2):
-            for c in range(2):
-                cols = slice(c * CHUNK, (c + 1) * CHUNK)
-                for t in range(PACK):
-                    ms = slice(t * P, (t + 1) * P)
-                    nc.tensor.matmul_mx(
-                        out=z[c][t][:], lhsT=wa_q[a][0][:, ms].bitcast(FP8X4), lhsT_scale=wa_q[a][1][:, ms],
-                        rhs=v_w[a][:, cols].bitcast(FP8X4), rhs_scale=v_sc[4 + 4 * a:, cols],
-                        start=(a == 0), stop=False,
-                    )
+
+        def paper_pass(a, t, c, stop):
+            ms, cols = slice(t * P, (t + 1) * P), slice(c * CHUNK, (c + 1) * CHUNK)
+            nc.tensor.matmul_mx(
+                out=z[c][t][:], lhsT=wa_q[a][0][:, ms].bitcast(FP8X4), lhsT_scale=wa_q[a][1][:, ms],
+                rhs=v_w[a][:, cols].bitcast(FP8X4), rhs_scale=v_sc[4 + 4 * a:, cols], start=(a == 0), stop=stop,
+            )
+
+        def citer_pass(t, c, stop):
+            ms, cols = slice(t * P, (t + 1) * P), slice(c * CHUNK, (c + 1) * CHUNK)
+            nc.tensor.matmul_mx(
+                out=z[c][t][:], lhsT=wb_w[:, 2 * t * P:2 * (t + 1) * P].bitcast(FP4X4), lhsT_scale=wb_sc[:, ms],
+                rhs=v2_w[:, cols].bitcast(FP8X4), rhs_scale=v2_sc[:, cols], start=False, stop=stop,
+            )
+
         for t in range(PACK):
-            ms = slice(t * P, (t + 1) * P)
             for c in range(2):
-                cols = slice(c * CHUNK, (c + 1) * CHUNK)
-                nc.tensor.matmul_mx(
-                    out=z[c][t][:], lhsT=wb_w[:, 2 * t * P:2 * (t + 1) * P].bitcast(FP4X4), lhsT_scale=wb_sc[:, ms],
-                    rhs=v2_w[:, cols].bitcast(FP8X4), rhs_scale=v2_sc[:, cols],
-                    start=False, stop=True,
-                )
-                nc.scalar.copy(z_sb[:, t, cols], z[c][t][:])
+                paper_pass(0, t, c, False)
+        for t in range(PACK):
+            for c in range(2):
+                if t < 2:
+                    paper_pass(1, t, c, False)
+                    citer_pass(t, c, True)
+                else:
+                    citer_pass(t, c, False)
+                    paper_pass(1, t, c, True)
+                nc.scalar.copy(z_sb[:, t, c * CHUNK:(c + 1) * CHUNK], z[c][t][:])
+        wm_w = work.tile([P, N], U32, name="wm_w", tag="v_w1", bufs=1, align_bytes=64)
+        for g in range(2):
+            nc.scalar.copy(
+                wm_w[:, g * PASS:(g + 1) * PASS].rearrange("p (t c i) -> p c t i", t=PACK, i=4),
+                wm_raw[:, g * PASS:(g + 1) * PASS].bitcast(U32).rearrange("p (c i t) -> p c t i", t=PACK, i=4),
+            )
 
         def slope(t, lo, hi):
             nc.vector.tensor_tensor(
@@ -279,7 +288,7 @@ def tile_list_citation_edge_gate_kernel(
             nc.vector.quantize_mx(out=y_w[:].bitcast(FP8X4), scales=y_sc[:, g, first:first + width], in_=staged[u][:])
             nc.sync.dma_start(words_of(out_1, g)[:, first:first + width], y_w[:].bitcast(I32))
         for r in range(4):
-            nc.scalar.dma_start(
+            (nc.scalar if r % 2 == 0 else nc.sync).dma_start(
                 out_2[:, r:16:4, :].bitcast(I32).rearrange("g q n -> q g n"),
                 y_sc[r:P:32, :, :].bitcast(I32),
             )

@@ -22,6 +22,7 @@ P = 128
 PACK = 4
 PASS = P * PACK
 CHUNK = 512
+SPREAD = 7
 
 
 def tile_list_citation_edge_gate_kernel(
@@ -51,6 +52,8 @@ def tile_list_citation_edge_gate_kernel(
         nc.gpsimd.memset(tab2_sc[:, :T].bitcast(I32), 0)
         nc.vector.memset(tab2_sc[:, T:].bitcast(I32), 0)
         nc.vector.memset(tab_sc[:].bitcast(I32), 0)
+        v2_sc = held([P, S], U8, "v2_sc")
+        nc.vector.memset(v2_sc[:].bitcast(I32), 0)
         nc.vector.memset(wb_sc_raw[:].bitcast(I32), 0)
         nc.vector.memset(wm_sc_raw[:].bitcast(I32), 0)
 
@@ -78,25 +81,34 @@ def tile_list_citation_edge_gate_kernel(
         wa_rows = wa.rearrange("(a p j) r -> a p j r", a=2, j=PACK)
         g_rows = gT.rearrange("(p t) c -> t p c", t=PACK)
         we_rows = we.rearrange("(p j) (g n) -> g p j n", j=PACK, g=2)
+
+        def load_tab_scales(queue):
+            for q in range(4):
+                queue.dma_start(
+                    tab_sc[32 * q + 4:32 * q + 12, :].bitcast(I32), tab_scales[:, 4 * q:4 * q + 4, :].bitcast(I32),
+                )
+
+        def load_wb_scales(queue):
+            for r in range(4):
+                queue.dma_start(wb_sc_raw[r:P:32, :].bitcast(I32), wb_scales[0, r:16:4, :].bitcast(I32))
+
+        def load_wm_scales(queue):
+            for q in range(4):
+                queue.dma_start(
+                    wm_sc_raw[32 * q + 8:32 * q + 16, :].bitcast(I32),
+                    wm_scales[0, 4 * q:4 * q + 4, :].bitcast(I32).rearrange("r (g n) -> g r n", g=2),
+                )
+
         nc.sync.dma_start(idx[:], offs)
         nc.sync.dma_start(tab_w[0][:], words_of(tab_words, 0))
         nc.sync.dma_start(idx2[:], offs2)
-        for r in range(4):
-            nc.sync.dma_start(tab2_sc[r:P:32, :].bitcast(I32), tab2_scales[0, r:16:4, :].bitcast(I32))
-        for q in range(4):
-            nc.gpsimd.dma_start(
-                tab_sc[32 * q + 4:32 * q + 12, :].bitcast(I32), tab_scales[:, 4 * q:4 * q + 4, :].bitcast(I32),
-            )
-        for r in range(4):
-            nc.gpsimd.dma_start(wb_sc_raw[r:P:32, :].bitcast(I32), wb_scales[0, r:16:4, :].bitcast(I32))
-        for q in range(4):
-            nc.gpsimd.dma_start(
-                wm_sc_raw[32 * q:32 * q + 8, :].bitcast(I32),
-                wm_scales[0, 4 * q:4 * q + 4, :].bitcast(I32).rearrange("r (g n) -> g r n", g=2),
-            )
+        nc.sync.dma_start(tab2_sc[0:16 * SPREAD:SPREAD, :].bitcast(I32), tab2_scales[0].bitcast(I32))
+        load_tab_scales(nc.gpsimd)
+        load_wb_scales(nc.gpsimd)
         nc.sync.dma_start(wa_raw[0][:], wa_rows[0])
         nc.sync.dma_start(wa_raw[1][:], wa_rows[1])
         nc.sync.dma_start(tab_w[1][:], words_of(tab_words, 1))
+        load_wm_scales(nc.sync)
         nc.sync.dma_start(tab2_w[:], words_of(tab2_words, 0))
         nc.sync.dma_start(wb_raw[:].bitcast(I32), wb_words[0].bitcast(I32))
         for t in range(PACK - 1):
@@ -113,9 +125,13 @@ def tile_list_citation_edge_gate_kernel(
         v_w = [work.tile([P, S], U32, name="v_w%d" % a, tag="v_w%d" % a, bufs=1, align_bytes=64) for a in range(2)]
         v_sc = early.tile([P, S], U8, name="v_sc", offset=T2 - S // 2, align_bytes=64)
         v2_w = held([P, S], U32, "v2_w")
-        v2_sc = held([P, S], U8, "v2_sc")
+        v2_spread = held([P, S], U8, "v2_spread")
         nc.vector.tensor_copy(v_w[0][:], tab_w[0][:].bitcast(U32).indirect(idx[:]))
-        nc.vector.tensor_copy(v2_sc[:], tab2_sc[:].indirect(idx2[:]))
+        nc.vector.tensor_copy(v2_spread[:], tab2_sc[:].indirect(idx2[:]))
+        for r in range(4):
+            nc.gpsimd.dma_start(
+                v2_sc[r:P:32, :].bitcast(I32), v2_spread[SPREAD * r:16 * SPREAD:4 * SPREAD, :].bitcast(I32),
+            )
         nc.vector.tensor_copy(v_sc[:], tab_sc[:].indirect(idx[:]))
         nc.vector.tensor_copy(v_w[1][:], tab_w[1][:].bitcast(U32).indirect(idx[:]))
 
@@ -245,7 +261,7 @@ def tile_list_citation_edge_gate_kernel(
                 m = bank("m", 1, width)
                 nc.tensor.matmul_mx(
                     out=m[:], lhsT=wm_w[:, g * PASS + t * P:g * PASS + (t + 1) * P].bitcast(FP8X4),
-                    lhsT_scale=wm_sc[4 * g:, ms],
+                    lhsT_scale=wm_sc[8 + 4 * g:, ms],
                     rhs=v2_w[:, cols].bitcast(FP8X4), rhs_scale=v2_sc[:, cols], start=True, stop=True,
                 )
                 nc.scalar.activation(y[:, t, :], e[:], SIGMOID, bias=bias[:, g, t:t + 1])

@@ -49,13 +49,10 @@ def tile_list_citation_edge_gate_kernel(
         tab2_sc = early.tile([P, T2], U8, name="tab2_sc", offset=0, align_bytes=64)
         wb_sc_raw = held([P, PASS], U8, "wb_sc_raw")
         wm_sc_raw = held([P, PASS], U8, "wm_sc_raw")
-        nc.gpsimd.memset(tab2_sc[:, :T].bitcast(I32), 0)
-        nc.vector.memset(tab2_sc[:, T:].bitcast(I32), 0)
-        nc.vector.memset(tab_sc[:].bitcast(I32), 0)
         v2_sc = held([P, S], U8, "v2_sc")
-        nc.vector.memset(v2_sc[:].bitcast(I32), 0)
-        nc.vector.memset(wb_sc_raw[:].bitcast(I32), 0)
-        nc.vector.memset(wm_sc_raw[:].bitcast(I32), 0)
+        nc.gpsimd.memset(tab_sc[:].bitcast(I32), 0)
+        for cleared in (tab2_sc, wb_sc_raw, wm_sc_raw, v2_sc):
+            nc.vector.memset(cleared[:].bitcast(I32), 0)
 
         def big(name, shape, dtype):
             return work.tile(shape, dtype, name=name, tag="big", bufs=5, align_bytes=64)
@@ -102,13 +99,13 @@ def tile_list_citation_edge_gate_kernel(
         nc.sync.dma_start(idx[:], offs)
         nc.sync.dma_start(tab_w[0][:], words_of(tab_words, 0))
         nc.sync.dma_start(idx2[:], offs2)
-        nc.sync.dma_start(tab2_sc[0:16 * SPREAD:SPREAD, :].bitcast(I32), tab2_scales[0].bitcast(I32))
         load_tab_scales(nc.gpsimd)
         load_wb_scales(nc.gpsimd)
+        load_wm_scales(nc.gpsimd)
         nc.sync.dma_start(wa_raw[0][:], wa_rows[0])
+        nc.sync.dma_start(tab2_sc[0:16 * SPREAD:SPREAD, :].bitcast(I32), tab2_scales[0].bitcast(I32))
         nc.sync.dma_start(wa_raw[1][:], wa_rows[1])
         nc.sync.dma_start(tab_w[1][:], words_of(tab_words, 1))
-        load_wm_scales(nc.sync)
         nc.sync.dma_start(tab2_w[:], words_of(tab2_words, 0))
         nc.sync.dma_start(wb_raw[:].bitcast(I32), wb_words[0].bitcast(I32))
         for t in range(PACK - 1):
@@ -128,10 +125,6 @@ def tile_list_citation_edge_gate_kernel(
         v2_spread = held([P, S], U8, "v2_spread")
         nc.vector.tensor_copy(v_w[0][:], tab_w[0][:].bitcast(U32).indirect(idx[:]))
         nc.vector.tensor_copy(v2_spread[:], tab2_sc[:].indirect(idx2[:]))
-        for r in range(4):
-            nc.gpsimd.dma_start(
-                v2_sc[r:P:32, :].bitcast(I32), v2_spread[SPREAD * r:16 * SPREAD:4 * SPREAD, :].bitcast(I32),
-            )
         nc.vector.tensor_copy(v_sc[:], tab_sc[:].indirect(idx[:]))
         nc.vector.tensor_copy(v_w[1][:], tab_w[1][:].bitcast(U32).indirect(idx[:]))
 
@@ -153,7 +146,12 @@ def tile_list_citation_edge_gate_kernel(
             nc.vector.quantize_mx(out=codes[:].bitcast(FP8X4), scales=scales[:], in_=staged)
             return codes, scales
 
-        wa_q = [quantise(round_weight(wa_raw[a], staging("wa_bf%d" % a)), "wa_q%d" % a) for a in range(2)]
+        wa_q = [quantise(round_weight(wa_raw[0], staging("wa_bf0")), "wa_q0")]
+        for r in range(4):
+            nc.scalar.dma_start(
+                v2_sc[r:P:32, :].bitcast(I32), v2_spread[SPREAD * r:16 * SPREAD:4 * SPREAD, :].bitcast(I32),
+            )
+        wa_q.append(quantise(round_weight(wa_raw[1], staging("wa_bf1")), "wa_q1"))
         wb_w = held([P, 2 * H], U8, "wb_w")
         nc.scalar.copy(
             wb_w[:].bitcast(U16).rearrange("p (t c i) -> p c t i", t=PACK, i=8),
@@ -185,31 +183,32 @@ def tile_list_citation_edge_gate_kernel(
 
         z = [[bank("z", c, CHUNK) for t in range(PACK)] for c in range(2)]
 
-        def paper_pass(a, t, c, stop):
+        def paper_pass(a, t, c, start, stop):
             ms, cols = slice(t * P, (t + 1) * P), slice(c * CHUNK, (c + 1) * CHUNK)
             nc.tensor.matmul_mx(
                 out=z[c][t][:], lhsT=wa_q[a][0][:, ms].bitcast(FP8X4), lhsT_scale=wa_q[a][1][:, ms],
-                rhs=v_w[a][:, cols].bitcast(FP8X4), rhs_scale=v_sc[4 + 4 * a:, cols], start=(a == 0), stop=stop,
+                rhs=v_w[a][:, cols].bitcast(FP8X4), rhs_scale=v_sc[4 + 4 * a:, cols], start=start, stop=stop,
             )
 
-        def citer_pass(t, c, stop):
+        def citer_pass(t, c, start, stop):
             ms, cols = slice(t * P, (t + 1) * P), slice(c * CHUNK, (c + 1) * CHUNK)
             nc.tensor.matmul_mx(
                 out=z[c][t][:], lhsT=wb_w[:, 2 * t * P:2 * (t + 1) * P].bitcast(FP4X4), lhsT_scale=wb_sc[:, ms],
-                rhs=v2_w[:, cols].bitcast(FP8X4), rhs_scale=v2_sc[:, cols], start=False, stop=stop,
+                rhs=v2_w[:, cols].bitcast(FP8X4), rhs_scale=v2_sc[:, cols], start=start, stop=stop,
             )
 
-        for t in range(PACK):
+        for t in range(2):
             for c in range(2):
-                paper_pass(0, t, c, False)
+                paper_pass(0, t, c, True, False)
         for t in range(PACK):
             for c in range(2):
                 if t < 2:
-                    paper_pass(1, t, c, False)
-                    citer_pass(t, c, True)
+                    paper_pass(1, t, c, False, False)
+                    citer_pass(t, c, False, True)
                 else:
-                    citer_pass(t, c, False)
-                    paper_pass(1, t, c, True)
+                    citer_pass(t, c, True, False)
+                    paper_pass(0, t, c, False, False)
+                    paper_pass(1, t, c, False, True)
                 nc.scalar.copy(z_sb[:, t, c * CHUNK:(c + 1) * CHUNK], z[c][t][:])
         wm_w = work.tile([P, N], U32, name="wm_w", tag="v_w1", bufs=1, align_bytes=64)
         for g in range(2):

@@ -50,9 +50,11 @@ def tile_list_citation_edge_gate_kernel(
         wb_sc_raw = held([P, PASS], U8, "wb_sc_raw")
         wm_sc_raw = held([P, PASS], U8, "wm_sc_raw")
         v2_sc = held([P, S], U8, "v2_sc")
+        warm = held([P, 2], F32, "warm")
         nc.gpsimd.memset(tab_sc[:].bitcast(I32), 0)
         for cleared in (tab2_sc, wb_sc_raw, wm_sc_raw, v2_sc):
             nc.vector.memset(cleared[:].bitcast(I32), 0)
+        nc.vector.memset(warm[:, 0:1], 0.0)
 
         def big(name, shape, dtype):
             return work.tile(shape, dtype, name=name, tag="big", bufs=5, align_bytes=64)
@@ -108,16 +110,14 @@ def tile_list_citation_edge_gate_kernel(
         nc.sync.dma_start(tab_w[1][:], words_of(tab_words, 1))
         nc.sync.dma_start(tab2_w[:], words_of(tab2_words, 0))
         nc.sync.dma_start(wb_raw[:].bitcast(I32), wb_words[0].bitcast(I32))
-        for t in range(PACK - 1):
+        for t in range(PACK):
             nc.sync.dma_start(g_win[t][:], g_rows[t])
         nc.sync.dma_start(wm_raw[:], words_of(wm_words, 0))
-        nc.sync.dma_start(g_win[PACK - 1][:], g_rows[PACK - 1])
-        nc.sync.dma_start(bias[:], be.rearrange("(g p t) -> p g t", g=2, t=PACK))
         nc.sync.dma_start(we_raw[0][:], we_rows[0])
         nc.sync.dma_start(we_raw[1][:], we_rows[1])
+        nc.sync.dma_start(bias[:], be.rearrange("(g p t) -> p g t", g=2, t=PACK))
 
-        warm = held([P, 1], F32, "warm")
-        nc.scalar.activation(warm[:], wa_raw[0][:, 0, 0:1], SIGMOID)
+        nc.scalar.activation(warm[:, 1:2], warm[:, 0:1], SIGMOID)
 
         v_w = [work.tile([P, S], U32, name="v_w%d" % a, tag="v_w%d" % a, bufs=1, align_bytes=64) for a in range(2)]
         v_sc = early.tile([P, S], U8, name="v_sc", offset=T2 - S // 2, align_bytes=64)

@@ -22,6 +22,7 @@ P = 128
 PACK = 4
 PASS = P * PACK
 CHUNK = 512
+QUARTER = 256
 SPREAD = 7
 
 
@@ -35,6 +36,8 @@ def tile_list_citation_edge_gate_kernel(
         work = ctx.enter_context(tc.tile_pool(name="work", bufs=1))
         reused = ctx.enter_context(tc.tile_pool(name="reused", bufs=1))
         early = ctx.enter_context(tc.tile_pool(name="early", bufs=1))
+        second = ctx.enter_context(tc.tile_pool(name="second", bufs=1))
+        late = ctx.enter_context(tc.tile_pool(name="late", bufs=1))
         psum = ctx.enter_context(tc.psum_pool(name="psum", bufs=1))
 
         def held(shape, dtype, name):
@@ -57,7 +60,7 @@ def tile_list_citation_edge_gate_kernel(
         nc.vector.memset(warm[:, 0:1], 0.0)
 
         def big(name, shape, dtype):
-            return work.tile(shape, dtype, name=name, tag="big", bufs=5, align_bytes=64)
+            return work.tile(shape, dtype, name=name, tag="big", bufs=4, align_bytes=64)
 
         tab_w = [
             early.tile([P, T], I32, name="tab_w0", offset=T2, align_bytes=64),
@@ -67,7 +70,7 @@ def tile_list_citation_edge_gate_kernel(
         g_win = [held([P, T], F32, "g_win%d" % t) for t in range(PACK)]
         wa_raw = [
             big("wa_raw0", [P, PACK, PASS], F32),
-            work.tile([P, PACK, PASS], F32, name="wa_raw1", tag="wa_raw1", bufs=1, align_bytes=64),
+            second.tile([P, PACK, PASS], F32, name="wa_raw1", offset=0, align_bytes=64),
         ]
         we_raw = [
             reused.tile([P, PACK, PASS], F32, name="we_raw0", offset=0, align_bytes=64),
@@ -112,8 +115,8 @@ def tile_list_citation_edge_gate_kernel(
         nc.sync.dma_start(wb_raw[:].bitcast(I32), wb_words[0].bitcast(I32))
         for t in range(PACK):
             nc.sync.dma_start(g_win[t][:], g_rows[t])
-        nc.sync.dma_start(wm_raw[:], words_of(wm_words, 0))
         nc.sync.dma_start(we_raw[0][:], we_rows[0])
+        nc.sync.dma_start(wm_raw[:], words_of(wm_words, 0))
         nc.sync.dma_start(we_raw[1][:], we_rows[1])
         nc.sync.dma_start(bias[:], be.rearrange("(g p t) -> p g t", g=2, t=PACK))
 
@@ -165,15 +168,13 @@ def tile_list_citation_edge_gate_kernel(
             )
             return dealt
 
-        wb_sc = deal_scales(work.tile([P, PASS], U8, name="wb_sc", tag="wa_raw1", bufs=1, align_bytes=64), wb_sc_raw)
-        for c in range(2):
+        wb_sc = deal_scales(second.tile([P, PASS], U8, name="wb_sc", offset=0, align_bytes=64), wb_sc_raw)
+        wm_sc = deal_scales(second.tile([P, PASS], U8, name="wm_sc", offset=PASS, align_bytes=64), wm_sc_raw)
+        for lo in range(0, S, QUARTER):
             nc.vector.tensor_copy(
-                v2_w[:, c * CHUNK:(c + 1) * CHUNK],
-                tab2_w[:].bitcast(U32).indirect(idx2[:, c * CHUNK // 16:(c + 1) * CHUNK // 16]),
+                v2_w[:, lo:lo + QUARTER], tab2_w[:].bitcast(U32).indirect(idx2[:, lo // 16:(lo + QUARTER) // 16]),
             )
 
-
-        wm_sc = deal_scales(work.tile([P, PASS], U8, name="wm_sc", tag="tab2_w", bufs=1, align_bytes=64), wm_sc_raw)
 
         z_sb = held([P, PACK, S], F32, "z_sb")
         gz = held([P, PACK, S], F32, "gz")
@@ -181,35 +182,39 @@ def tile_list_citation_edge_gate_kernel(
         def bank(name, c, width):
             return psum.tile([P, width], F32, name=name, tag="bank%d" % c, bufs=4)
 
-        z = [[bank("z", c, CHUNK) for t in range(PACK)] for c in range(2)]
+        pieces = [(t, lo, QUARTER if t == 0 else CHUNK) for t in range(PACK) for lo in range(0, S, QUARTER if t == 0 else CHUNK)]
+        z = [bank("z", k % 2, width) for k, (t, lo, width) in enumerate(pieces[:8])]
 
-        def paper_pass(a, t, c, start, stop):
-            ms, cols = slice(t * P, (t + 1) * P), slice(c * CHUNK, (c + 1) * CHUNK)
+        def paper_pass(a, k, start, stop):
+            t, lo, width = pieces[k]
+            ms, cols = slice(t * P, (t + 1) * P), slice(lo, lo + width)
             nc.tensor.matmul_mx(
-                out=z[c][t][:], lhsT=wa_q[a][0][:, ms].bitcast(FP8X4), lhsT_scale=wa_q[a][1][:, ms],
+                out=z[k][:], lhsT=wa_q[a][0][:, ms].bitcast(FP8X4), lhsT_scale=wa_q[a][1][:, ms],
                 rhs=v_w[a][:, cols].bitcast(FP8X4), rhs_scale=v_sc[4 + 4 * a:, cols], start=start, stop=stop,
             )
 
-        def citer_pass(t, c, start, stop):
-            ms, cols = slice(t * P, (t + 1) * P), slice(c * CHUNK, (c + 1) * CHUNK)
+        def citer_pass(k, start, stop):
+            t, lo, width = pieces[k]
+            ms, cols = slice(t * P, (t + 1) * P), slice(lo, lo + width)
             nc.tensor.matmul_mx(
-                out=z[c][t][:], lhsT=wb_w[:, 2 * t * P:2 * (t + 1) * P].bitcast(FP4X4), lhsT_scale=wb_sc[:, ms],
+                out=z[k][:], lhsT=wb_w[:, 2 * t * P:2 * (t + 1) * P].bitcast(FP4X4), lhsT_scale=wb_sc[:, ms],
                 rhs=v2_w[:, cols].bitcast(FP8X4), rhs_scale=v2_sc[:, cols], start=start, stop=stop,
             )
 
-        for t in range(2):
-            for c in range(2):
-                paper_pass(0, t, c, True, False)
-        for t in range(PACK):
-            for c in range(2):
-                if t < 2:
-                    paper_pass(1, t, c, False, False)
-                    citer_pass(t, c, False, True)
-                else:
-                    citer_pass(t, c, True, False)
-                    paper_pass(0, t, c, False, False)
-                    paper_pass(1, t, c, False, True)
-                nc.scalar.copy(z_sb[:, t, c * CHUNK:(c + 1) * CHUNK], z[c][t][:])
+        for k, (t, lo, width) in enumerate(pieces):
+            if t < 2:
+                paper_pass(0, k, True, False)
+        for k, (t, lo, width) in enumerate(pieces):
+            if k >= len(z):
+                z.append(bank("z", k % 2, width))
+            if t < 2:
+                paper_pass(1, k, False, False)
+                citer_pass(k, False, True)
+            else:
+                citer_pass(k, True, False)
+                paper_pass(0, k, False, False)
+                paper_pass(1, k, False, True)
+            nc.scalar.copy(z_sb[:, t, lo:lo + width], z[k][:])
         wm_w = work.tile([P, N], U32, name="wm_w", tag="v_w1", bufs=1, align_bytes=64)
         for g in range(2):
             nc.scalar.copy(
@@ -232,7 +237,7 @@ def tile_list_citation_edge_gate_kernel(
             return h_bf
 
         for t in range(PACK):
-            width = CHUNK if t in (0, PACK - 1) else S
+            width = (QUARTER, S, S, CHUNK)[t]
             for lo in range(0, S, width):
                 slope(t, lo, lo + width)
 
@@ -246,27 +251,26 @@ def tile_list_citation_edge_gate_kernel(
         y_sc = held([P, 2, S], U8, "y_sc")
         y_rows = out_0.rearrange("(g p t) j -> g p t j", g=2, t=PACK)
 
-        def second_stage(y, g, first, width, slices, rows):
-            c, inner = divmod(first, CHUNK)
-            cols = slice(first, first + width)
-            within = slice(inner, inner + width)
-            for t in slices:
-                ms = slice(t * P, (t + 1) * P)
-                e = bank("e", 0, width)
-                nc.tensor.matmul_mx(
-                    out=e[:], lhsT=we_q[g][0][:, ms].bitcast(FP8X4), lhsT_scale=we_q[g][1][:, ms],
-                    rhs=h_q[c][0][:, within].bitcast(FP8X4), rhs_scale=h_q[c][1][:, within], start=True, stop=True,
-                )
-                m = bank("m", 1, width)
-                nc.tensor.matmul_mx(
-                    out=m[:], lhsT=wm_w[:, g * PASS + t * P:g * PASS + (t + 1) * P].bitcast(FP8X4),
-                    lhsT_scale=wm_sc[8 + 4 * g:, ms],
-                    rhs=v2_w[:, cols].bitcast(FP8X4), rhs_scale=v2_sc[:, cols], start=True, stop=True,
-                )
-                nc.scalar.activation(y[:, t, :], e[:], SIGMOID, bias=bias[:, g, t:t + 1])
-                nc.vector.tensor_tensor(y[:, t, :], m[:], y[:, t, :], MULT)
-                if (t + 1) % rows == 0:
-                    nc.sync.dma_start(y_rows[g][:, t + 1 - rows:t + 1, cols], y[:, t + 1 - rows:t + 1, :])
+        first_gate = reused.tile([P, CHUNK], F32, name="first_gate", offset=5120, align_bytes=64)
+        late_gate = late.tile([P, CHUNK], F32, name="late_gate", offset=0, align_bytes=64)
+        gates = {(0, 0, 0): first_gate, (0, 1, 2): late_gate}
+
+        def gated(y, g, c, t):
+            ms, cols = slice(t * P, (t + 1) * P), slice(c * CHUNK, (c + 1) * CHUNK)
+            e = bank("e", 0, CHUNK)
+            nc.tensor.matmul_mx(
+                out=e[:], lhsT=we_q[g][0][:, ms].bitcast(FP8X4), lhsT_scale=we_q[g][1][:, ms],
+                rhs=h_q[c][0][:].bitcast(FP8X4), rhs_scale=h_q[c][1][:], start=True, stop=True,
+            )
+            m = bank("m", 1, CHUNK)
+            nc.tensor.matmul_mx(
+                out=m[:], lhsT=wm_w[:, g * PASS + t * P:g * PASS + (t + 1) * P].bitcast(FP8X4),
+                lhsT_scale=wm_sc[8 + 4 * g:, ms],
+                rhs=v2_w[:, cols].bitcast(FP8X4), rhs_scale=v2_sc[:, cols], start=True, stop=True,
+            )
+            gate = gates[g, c, t][:] if (g, c, t) in gates else y
+            nc.scalar.activation(gate, e[:], SIGMOID, bias=bias[:, g, t:t + 1])
+            nc.vector.tensor_tensor(y, m[:], gate, MULT)
 
         def round_on_gpsimd(y_bf, y):
             nc.gpsimd.tensor_scalar(
@@ -278,30 +282,53 @@ def tile_list_citation_edge_gate_kernel(
                 y_bf.rearrange("p (c i t) -> p c t i", i=2, t=PACK), y.rearrange("p t (c i) -> p c t i", i=2),
             )
 
+        def round_on_vector(y_bf, y):
+            nc.vector.tensor_copy(
+                y_bf.rearrange("p (c i t) -> p c t i", i=4, t=PACK), y.rearrange("p t (c i) -> p c t i", i=4),
+            )
+
         half = CHUNK // 2
+        y_first = big("y_first", [P, PACK, CHUNK], F32)
+        y_wide = held([P, PACK, S], F32, "y_wide")
+        y_last = big("y_last", [P, PACK, CHUNK], F32)
+        for t in range(PACK):
+            gated(y_first[:, t, :], 0, 0, t)
+            nc.sync.dma_start(y_rows[0][:, t, 0:CHUNK], y_first[:, t, :])
+        h_q1_sc = reused.tile([P, PASS], U8, name="h_q1_sc", offset=5120, align_bytes=64)
+        h_q.append(quantise(h_bf1, "h_q1", h_q1_sc))
+        gated(y_wide[:, 0, 0:CHUNK], 1, 0, 0)
+        for t in range(PACK):
+            if t + 1 < PACK:
+                gated(y_wide[:, t + 1, 0:CHUNK], 1, 0, t + 1)
+            gated(y_wide[:, t, CHUNK:S], 1, 1, t)
+            nc.sync.dma_start(y_rows[1][:, t, :], y_wide[:, t, :])
+        for t in range(PACK):
+            gated(y_last[:, t, :], 0, 1, t)
+            if t % 2 == 1:
+                nc.sync.dma_start(y_rows[0][:, t - 1:t + 1, CHUNK:S], y_last[:, t - 1:t + 1, :])
         units = [
-            (0, 0, CHUNK, [(round_on_gpsimd, 0, half), (round_on_gpsimd, half, CHUNK)]),
-            (1, 0, CHUNK, [(round_on_gpsimd, 0, half), (round_on_gpsimd, half, CHUNK)]),
-            (0, CHUNK, CHUNK, [(round_on_gpsimd, 0, half // 2), (round_on_scalar, half // 2, CHUNK)]),
-            (1, CHUNK, half, [(round_on_scalar, 0, half)]),
-            (1, CHUNK + half, half, [(round_on_scalar, 0, half)]),
+            (0, 0, y_first[:], [(round_on_gpsimd, 0, CHUNK)]),
+            (1, 0, y_wide[:, :, 0:CHUNK], [(round_on_gpsimd, 0, CHUNK)]),
+            (1, 1, y_wide[:, :, CHUNK:S], [(round_on_scalar, 0, CHUNK)]),
+            (0, 1, y_last[:], [(round_on_scalar, 0, half), (round_on_vector, half, CHUNK)]),
         ]
-        ys = [big("y", [P, PACK, width], F32) for g, first, width, shares in units]
-        second_stage(ys[0], 0, 0, CHUNK, range(2), 1)
-        h_q.append(quantise(h_bf1, "h_q1"))
-        second_stage(ys[0], 0, 0, CHUNK, range(2, PACK), 1)
-        for u, (g, first, width, shares) in enumerate(units[1:]):
-            second_stage(ys[u + 1], g, first, width, range(PACK), 2)
         staged = []
-        for u, (g, first, width, shares) in enumerate(units):
-            y_bf = held([P, width * PACK], BF16, "y_bf%d" % u)
+        for u, (g, c, y, shares) in enumerate(units):
+            if u == 0:
+                y_bf = reused.tile([P, CHUNK * PACK], BF16, name="y_bf0", offset=0, align_bytes=64)
+            else:
+                y_bf = late.tile([P, CHUNK * PACK], BF16, name="y_bf%d" % u, offset=u * 2 * CHUNK * PACK, align_bytes=64)
             for rounder, lo, hi in shares:
-                rounder(y_bf[:, lo * PACK:hi * PACK], ys[u][:, :, lo:hi])
+                rounder(y_bf[:, lo * PACK:hi * PACK], y[:, :, lo:hi])
             staged.append(y_bf)
-        for u, (g, first, width, shares) in enumerate(units):
-            y_w = held([P, width], U32, "y_w%d" % u)
-            nc.vector.quantize_mx(out=y_w[:].bitcast(FP8X4), scales=y_sc[:, g, first:first + width], in_=staged[u][:])
-            nc.sync.dma_start(words_of(out_1, g)[:, first:first + width], y_w[:].bitcast(I32))
+        for u, (g, c, y, shares) in enumerate(units):
+            cols = slice(c * CHUNK, (c + 1) * CHUNK)
+            if u in (0, 3):
+                y_w = late.tile([P, CHUNK], U32, name="y_w%d" % u, offset=0 if u == 0 else 2 * CHUNK * PACK, align_bytes=64)
+            else:
+                y_w = held([P, CHUNK], U32, "y_w%d" % u)
+            nc.vector.quantize_mx(out=y_w[:].bitcast(FP8X4), scales=y_sc[:, g, cols], in_=staged[u][:])
+            nc.sync.dma_start(words_of(out_1, g)[:, cols], y_w[:].bitcast(I32))
         for r in range(4):
             (nc.scalar if r % 2 == 0 else nc.sync).dma_start(
                 out_2[:, r:16:4, :].bitcast(I32).rearrange("g q n -> q g n"),

from contextlib import ExitStack

import concourse.mybir as mybir

K, K2, T, T2, S, H, N = 1024, 512, 2048, 4096, 1024, 512, 1024
FLOPS = 2 * S * (K * H + K2 * H + H * N + K2 * N)

F32 = mybir.dt.float32
BF16 = mybir.dt.bfloat16
I32 = mybir.dt.int32
U32 = mybir.dt.uint32
U16 = mybir.dt.uint16
U8 = mybir.dt.uint8
FP8X4 = mybir.dt.float8_e4m3fn_x4
FP4X4 = mybir.dt.float4_e2m1fn_x4
MULT = mybir.AluOpType.mult
MAX = mybir.AluOpType.max
ADD = mybir.AluOpType.add
SIGMOID = mybir.ActivationFunctionType.Sigmoid

P = 128
PACK = 4
PASS = P * PACK
CHUNK = 512
QUARTER = 256
SPREAD = 7


def tile_list_citation_edge_gate_kernel(
    tc, tab_words, tab_scales, tab2_words, tab2_scales, wa, wb_words, wb_scales,
    wm_words, wm_scales, we, be, gT, offs, offs2, out_0, out_1, out_2,
):
    nc = tc.nc
    with ExitStack() as ctx:
        keep = ctx.enter_context(tc.tile_pool(name="keep", bufs=1))
        work = ctx.enter_context(tc.tile_pool(name="work", bufs=1))
        reused = ctx.enter_context(tc.tile_pool(name="reused", bufs=1))
        early = ctx.enter_context(tc.tile_pool(name="early", bufs=1))
        second = ctx.enter_context(tc.tile_pool(name="second", bufs=1))
        late = ctx.enter_context(tc.tile_pool(name="late", bufs=1))
        psum = ctx.enter_context(tc.psum_pool(name="psum", bufs=1))

        def held(shape, dtype, name):
            return keep.tile(shape, dtype, name=name, align_bytes=64)

        def words_of(dram, a):
            return dram[a].rearrange("p t i -> p (t i)").bitcast(I32)

        idx = keep.tile([P, S // 16], U16, name="idx")
        idx2 = keep.tile([P, S // 16], U16, name="idx2")
        tab_sc = held([P, T], U8, "tab_sc")
        tab2_sc = early.tile([P, T2], U8, name="tab2_sc", offset=0, align_bytes=64)
        wb_sc_raw = held([P, PASS], U8, "wb_sc_raw")
        wm_sc_raw = held([P, PASS], U8, "wm_sc_raw")
        v2_sc = held([P, S], U8, "v2_sc")
        warm = held([P, 2], F32, "warm")
        nc.gpsimd.memset(tab_sc[:].bitcast(I32), 0)
        for cleared in (tab2_sc, wb_sc_raw, wm_sc_raw, v2_sc):
            nc.vector.memset(cleared[:].bitcast(I32), 0)
        nc.vector.memset(warm[:, 0:1], 0.0)

        def big(name, shape, dtype):
            return work.tile(shape, dtype, name=name, tag="big", bufs=4, align_bytes=64)

        tab_w = [
            early.tile([P, T], I32, name="tab_w0", offset=T2, align_bytes=64),
            big("tab_w1", [P, T], I32),
        ]
        tab2_w = work.tile([P, T2], I32, name="tab2_w", tag="tab2_w", bufs=1, align_bytes=64)
        g_win = [held([P, T], F32, "g_win%d" % t) for t in range(PACK)]
        wa_raw = [
            big("wa_raw0", [P, PACK, PASS], F32),
            second.tile([P, PACK, PASS], F32, name="wa_raw1", offset=0, align_bytes=64),
        ]
        we_raw = [
            reused.tile([P, PACK, PASS], F32, name="we_raw0", offset=0, align_bytes=64),
            big("we_raw1", [P, PACK, PASS], F32),
        ]
        wb_raw = held([P, 2 * H], U8, "wb_raw")
        wm_raw = held([P, N], I32, "wm_raw")
        bias = held([P, 2, PACK], F32, "bias")

        wa_rows = wa.rearrange("(a p j) r -> a p j r", a=2, j=PACK)
        g_rows = gT.rearrange("(p t) c -> t p c", t=PACK)
        we_rows = we.rearrange("(p j) (g n) -> g p j n", j=PACK, g=2)

        def load_tab_scales(queue):
            for q in range(4):
                queue.dma_start(
                    tab_sc[32 * q + 4:32 * q + 12, :].bitcast(I32), tab_scales[:, 4 * q:4 * q + 4, :].bitcast(I32),
                )

        def load_wb_scales(queue):
            for r in range(4):
                queue.dma_start(wb_sc_raw[r:P:32, :].bitcast(I32), wb_scales[0, r:16:4, :].bitcast(I32))

        def load_wm_scales(queue):
            for q in range(4):
                queue.dma_start(
                    wm_sc_raw[32 * q + 8:32 * q + 16, :].bitcast(I32),
                    wm_scales[0, 4 * q:4 * q + 4, :].bitcast(I32).rearrange("r (g n) -> g r n", g=2),
                )

        nc.sync.dma_start(idx[:], offs)
        nc.sync.dma_start(tab_w[0][:], words_of(tab_words, 0))
        nc.sync.dma_start(idx2[:], offs2)
        load_tab_scales(nc.gpsimd)
        load_wb_scales(nc.gpsimd)
        load_wm_scales(nc.gpsimd)
        nc.sync.dma_start(wa_raw[0][:], wa_rows[0])
        nc.sync.dma_start(tab2_sc[0:16 * SPREAD:SPREAD, :].bitcast(I32), tab2_scales[0].bitcast(I32))
        nc.sync.dma_start(wa_raw[1][:], wa_rows[1])
        nc.sync.dma_start(tab_w[1][:], words_of(tab_words, 1))
        nc.sync.dma_start(tab2_w[:], words_of(tab2_words, 0))
        nc.sync.dma_start(wb_raw[:].bitcast(I32), wb_words[0].bitcast(I32))
        for t in range(PACK):
            nc.sync.dma_start(g_win[t][:], g_rows[t])
        nc.sync.dma_start(we_raw[0][:], we_rows[0])
        nc.sync.dma_start(wm_raw[:], words_of(wm_words, 0))
        nc.sync.dma_start(we_raw[1][:], we_rows[1])
        nc.sync.dma_start(bias[:], be.rearrange("(g p t) -> p g t", g=2, t=PACK))

        nc.scalar.activation(warm[:, 1:2], warm[:, 0:1], SIGMOID)

        v_w = [work.tile([P, S], U32, name="v_w%d" % a, tag="v_w%d" % a, bufs=1, align_bytes=64) for a in range(2)]
        v_sc = early.tile([P, S], U8, name="v_sc", offset=T2 - S // 2, align_bytes=64)
        v2_w = held([P, S], U32, "v2_w")
        v2_spread = held([P, S], U8, "v2_spread")
        nc.vector.tensor_copy(v_w[0][:], tab_w[0][:].bitcast(U32).indirect(idx[:]))
        nc.vector.tensor_copy(v2_spread[:], tab2_sc[:].indirect(idx2[:]))
        nc.vector.tensor_copy(v_sc[:], tab_sc[:].indirect(idx[:]))
        nc.vector.tensor_copy(v_w[1][:], tab_w[1][:].bitcast(U32).indirect(idx[:]))

        def staging(name):
            return work.tile([P, PASS * PACK], BF16, name=name, tag="staged", bufs=3, align_bytes=64)[:]

        def round_weight(raw, staged):
            for u in range(2):
                nc.scalar.copy(
                    staged.rearrange("p (u e m j) -> p u m j e", u=2, e=2, j=PACK)[:, u],
                    raw[:].rearrange("p j (m u e) -> p u m j e", u=2, e=2)[:, u],
                )
            return staged

        def quantise(staged, name, scales=None):
            codes = held([P, PASS], U32, name + "_w")
            if scales is None:
                scales = held([P, PASS], U8, name + "_sc")
            nc.vector.quantize_mx(out=codes[:].bitcast(FP8X4), scales=scales[:], in_=staged)
            return codes, scales

        wa_q = [quantise(round_weight(wa_raw[0], staging("wa_bf0")), "wa_q0")]
        for r in range(4):
            nc.scalar.dma_start(
                v2_sc[r:P:32, :].bitcast(I32), v2_spread[SPREAD * r:16 * SPREAD:4 * SPREAD, :].bitcast(I32),
            )
        wa_q.append(quantise(round_weight(wa_raw[1], staging("wa_bf1")), "wa_q1"))
        wb_w = held([P, 2 * H], U8, "wb_w")
        nc.scalar.copy(
            wb_w[:].bitcast(U16).rearrange("p (t c i) -> p c t i", t=PACK, i=8),
            wb_raw[:].bitcast(U16).rearrange("p (c i t) -> p c t i", t=PACK, i=8),
        )

        def deal_scales(dealt, raw):
            nc.vector.tensor_copy(
                dealt[:].rearrange("p (t c i) -> p c t i", t=PACK, i=16),
                raw[:].rearrange("p (c i t) -> p c t i", t=PACK, i=16),
            )
            return dealt

        wb_sc = deal_scales(second.tile([P, PASS], U8, name="wb_sc", offset=0, align_bytes=64), wb_sc_raw)
        wm_sc = deal_scales(second.tile([P, PASS], U8, name="wm_sc", offset=PASS, align_bytes=64), wm_sc_raw)
        for lo in range(0, S, QUARTER):
            nc.vector.tensor_copy(
                v2_w[:, lo:lo + QUARTER], tab2_w[:].bitcast(U32).indirect(idx2[:, lo // 16:(lo + QUARTER) // 16]),
            )


        z_sb = held([P, PACK, S], F32, "z_sb")
        gz = held([P, PACK, S], F32, "gz")

        def bank(name, c, width):
            return psum.tile([P, width], F32, name=name, tag="bank%d" % c, bufs=4)

        pieces = [(t, lo, QUARTER if t == 0 else CHUNK) for t in range(PACK) for lo in range(0, S, QUARTER if t == 0 else CHUNK)]
        z = [bank("z", k % 2, width) for k, (t, lo, width) in enumerate(pieces[:8])]

        def paper_pass(a, k, start, stop):
            t, lo, width = pieces[k]
            ms, cols = slice(t * P, (t + 1) * P), slice(lo, lo + width)
            nc.tensor.matmul_mx(
                out=z[k][:], lhsT=wa_q[a][0][:, ms].bitcast(FP8X4), lhsT_scale=wa_q[a][1][:, ms],
                rhs=v_w[a][:, cols].bitcast(FP8X4), rhs_scale=v_sc[4 + 4 * a:, cols], start=start, stop=stop,
            )

        def citer_pass(k, start, stop):
            t, lo, width = pieces[k]
            ms, cols = slice(t * P, (t + 1) * P), slice(lo, lo + width)
            nc.tensor.matmul_mx(
                out=z[k][:], lhsT=wb_w[:, 2 * t * P:2 * (t + 1) * P].bitcast(FP4X4), lhsT_scale=wb_sc[:, ms],
                rhs=v2_w[:, cols].bitcast(FP8X4), rhs_scale=v2_sc[:, cols], start=start, stop=stop,
            )

        for k, (t, lo, width) in enumerate(pieces):
            if t < 2:
                paper_pass(0, k, True, False)
        for k, (t, lo, width) in enumerate(pieces):
            if k >= len(z):
                z.append(bank("z", k % 2, width))
            if t < 2:
                paper_pass(1, k, False, False)
                citer_pass(k, False, True)
            else:
                citer_pass(k, True, False)
                paper_pass(0, k, False, False)
                paper_pass(1, k, False, True)
            nc.scalar.copy(z_sb[:, t, lo:lo + width], z[k][:])
        wm_w = work.tile([P, N], U32, name="wm_w", tag="v_w1", bufs=1, align_bytes=64)
        for g in range(2):
            nc.scalar.copy(
                wm_w[:, g * PASS:(g + 1) * PASS].rearrange("p (t c i) -> p c t i", t=PACK, i=4),
                wm_raw[:, g * PASS:(g + 1) * PASS].bitcast(U32).rearrange("p (c i t) -> p c t i", t=PACK, i=4),
            )

        def slope(t, lo, hi):
            nc.vector.tensor_tensor(
                gz[:, t, lo:hi], g_win[t][:].indirect(idx[:, lo // 16:hi // 16]), z_sb[:, t, lo:hi], MULT,
            )

        def rectify(c, h_bf):
            nc.vector.tensor_tensor(
                h_bf.rearrange("p (c i t) -> p c t i", i=2, t=PACK),
                z_sb[:, :, c * CHUNK:(c + 1) * CHUNK].rearrange("p t (c i) -> p c t i", i=2),
                gz[:, :, c * CHUNK:(c + 1) * CHUNK].rearrange("p t (c i) -> p c t i", i=2),
                MAX,
            )
            return h_bf

        for t in range(PACK):
            width = (QUARTER, S, S, CHUNK)[t]
            for lo in range(0, S, width):
                slope(t, lo, lo + width)

        h_bf0 = rectify(0, staging("h_bf0"))
        we_q = [quantise(round_weight(we_raw[0], held([P, PASS * PACK], BF16, "we_bf0")[:]), "we_q0")]
        h_q0_sc = reused.tile([P, PASS], U8, name="h_q0_sc", offset=2 * PASS * PACK, align_bytes=64)
        h_q = [quantise(h_bf0, "h_q0", h_q0_sc)]
        h_bf1 = rectify(1, reused.tile([P, PASS * PACK], BF16, name="h_bf1", offset=0, align_bytes=64)[:])
        we_q.append(quantise(round_weight(we_raw[1], staging("we_bf1")), "we_q1"))

        y_sc = held([P, 2, S], U8, "y_sc")
        y_rows = out_0.rearrange("(g p t) j -> g p t j", g=2, t=PACK)

        first_gate = reused.tile([P, CHUNK], F32, name="first_gate", offset=5120, align_bytes=64)
        late_gate = late.tile([P, CHUNK], F32, name="late_gate", offset=0, align_bytes=64)
        gates = {(0, 0, 0): first_gate, (0, 1, 2): late_gate}

        def gated(y, g, c, t):
            ms, cols = slice(t * P, (t + 1) * P), slice(c * CHUNK, (c + 1) * CHUNK)
            e = bank("e", 0, CHUNK)
            nc.tensor.matmul_mx(
                out=e[:], lhsT=we_q[g][0][:, ms].bitcast(FP8X4), lhsT_scale=we_q[g][1][:, ms],
                rhs=h_q[c][0][:].bitcast(FP8X4), rhs_scale=h_q[c][1][:], start=True, stop=True,
            )
            m = bank("m", 1, CHUNK)
            nc.tensor.matmul_mx(
                out=m[:], lhsT=wm_w[:, g * PASS + t * P:g * PASS + (t + 1) * P].bitcast(FP8X4),
                lhsT_scale=wm_sc[8 + 4 * g:, ms],
                rhs=v2_w[:, cols].bitcast(FP8X4), rhs_scale=v2_sc[:, cols], start=True, stop=True,
            )
            gate = gates[g, c, t][:] if (g, c, t) in gates else y
            nc.scalar.activation(gate, e[:], SIGMOID, bias=bias[:, g, t:t + 1])
            nc.vector.tensor_tensor(y, m[:], gate, MULT)

        def round_on_gpsimd(y_bf, y):
            nc.gpsimd.tensor_scalar(
                y_bf.rearrange("p (c t) -> p c t", t=PACK), y.rearrange("p t c -> p c t"), 1.0, -0.0, MULT, ADD,
            )

        def round_on_scalar(y_bf, y):
            nc.scalar.copy(
                y_bf.rearrange("p (c i t) -> p c t i", i=2, t=PACK), y.rearrange("p t (c i) -> p c t i", i=2),
            )

        def round_on_vector(y_bf, y):
            nc.vector.tensor_copy(
                y_bf.rearrange("p (c i t) -> p c t i", i=4, t=PACK), y.rearrange("p t (c i) -> p c t i", i=4),
            )

        half = CHUNK // 2
        y_first = big("y_first", [P, PACK, CHUNK], F32)
        y_wide = held([P, PACK, S], F32, "y_wide")
        y_last = big("y_last", [P, PACK, CHUNK], F32)
        for t in range(PACK):
            gated(y_first[:, t, :], 0, 0, t)
            nc.sync.dma_start(y_rows[0][:, t, 0:CHUNK], y_first[:, t, :])
        h_q1_sc = reused.tile([P, PASS], U8, name="h_q1_sc", offset=5120, align_bytes=64)
        h_q.append(quantise(h_bf1, "h_q1", h_q1_sc))
        gated(y_wide[:, 0, 0:CHUNK], 1, 0, 0)
        for t in range(PACK):
            if t + 1 < PACK:
                gated(y_wide[:, t + 1, 0:CHUNK], 1, 0, t + 1)
            gated(y_wide[:, t, CHUNK:S], 1, 1, t)
            nc.sync.dma_start(y_rows[1][:, t, :], y_wide[:, t, :])
        for t in range(PACK):
            gated(y_last[:, t, :], 0, 1, t)
            if t % 2 == 1:
                nc.sync.dma_start(y_rows[0][:, t - 1:t + 1, CHUNK:S], y_last[:, t - 1:t + 1, :])
        units = [
            (0, 0, y_first[:], [(round_on_gpsimd, 0, CHUNK)]),
            (1, 0, y_wide[:, :, 0:CHUNK], [(round_on_gpsimd, 0, CHUNK)]),
            (1, 1, y_wide[:, :, CHUNK:S], [(round_on_scalar, 0, CHUNK)]),
            (0, 1, y_last[:], [(round_on_scalar, 0, half), (round_on_vector, half, CHUNK)]),
        ]
        staged = []
        for u, (g, c, y, shares) in enumerate(units):
            if u == 0:
                y_bf = reused.tile([P, CHUNK * PACK], BF16, name="y_bf0", offset=0, align_bytes=64)
            else:
                y_bf = late.tile([P, CHUNK * PACK], BF16, name="y_bf%d" % u, offset=u * 2 * CHUNK * PACK, align_bytes=64)
            for rounder, lo, hi in shares:
                rounder(y_bf[:, lo * PACK:hi * PACK], y[:, :, lo:hi])
            staged.append(y_bf)
        for u, (g, c, y, shares) in enumerate(units):
            cols = slice(c * CHUNK, (c + 1) * CHUNK)
            if u in (0, 3):
                y_w = late.tile([P, CHUNK], U32, name="y_w%d" % u, offset=0 if u == 0 else 2 * CHUNK * PACK, align_bytes=64)
            else:
                y_w = held([P, CHUNK], U32, "y_w%d" % u)
            nc.vector.quantize_mx(out=y_w[:].bitcast(FP8X4), scales=y_sc[:, g, cols], in_=staged[u][:])
            nc.sync.dma_start(words_of(out_1, g)[:, cols], y_w[:].bitcast(I32))
        for r in range(4):
            (nc.scalar if r % 2 == 0 else nc.sync).dma_start(
                out_2[:, r:16:4, :].bitcast(I32).rearrange("g q n -> q g n"),
                y_sc[r:P:32, :, :].bitcast(I32),
            )
